import numpy as np
import ml_dtypes


def mxq(x, axis, fmt="e4m3"):
    dtype, down = {"e4m3": (ml_dtypes.float8_e4m3fn, 7), "e5m2": (ml_dtypes.float8_e5m2, 14)}[fmt]
    v = np.moveaxis(np.asarray(x, np.float32).astype(ml_dtypes.bfloat16).astype(np.float64), axis, -1)
    blocks = v.reshape(v.shape[:-1] + (-1, 32))
    amax = np.abs(blocks).max(-1, keepdims=True)
    byte = np.maximum(np.where(amax > 0, np.frexp(amax)[1] - 1 + 127, 0) - down, 1)
    scale = np.exp2(byte - 127.0)
    codes = (blocks / scale).astype(np.float32).astype(dtype).astype(np.float64)
    return np.moveaxis((codes * scale).reshape(v.shape), -1, axis)


WIDE = False


def mx_kscale(k):
    if not WIDE:
        return np.ones(k)
    levels = np.array([10, -10, 5, -5, 0])
    if k % 512:
        return np.exp2(np.random.permutation(np.resize(levels, k // 32))).repeat(32)
    a = np.empty((k // 512, 16))
    for p in range(k // 512):
        a[p, :8] = np.random.permutation(np.resize(levels, 8))
        for g in range(8):
            far = levels[np.abs(levels - a[p, g]) >= 10]
            a[p, g + 8] = far[np.random.randint(len(far))]
    return np.exp2(a.ravel()).repeat(32)


def f64(x):
    return np.asarray(x).astype(np.float64)


def striped(idx):
    return np.tile(idx.reshape(-1, 16).T, (8, 1)).astype(np.uint16)


def unstriped(offs):
    return offs[:16].T.reshape(-1).astype(np.int64)


E2M1 = np.array([0.0, 0.5, 1.0, 1.5, 2.0, 3.0, 4.0, 6.0, -0.0, -0.5, -1.0, -1.5, -2.0, -3.0, -4.0, -6.0])


def pack_weight(w, fmt):
    k, n = w.shape
    w = f64(np.asarray(w, np.float32).astype(ml_dtypes.bfloat16)).reshape(k // 32, 32, n)
    amax = np.abs(w).max(1)
    if fmt == "e4m3":
        byte = np.frexp(amax)[1] - 1 + 127 - 7
    else:
        mant, ex = np.frexp(amax / 6.0)
        byte = np.where(mant > 0.5, ex, ex - 1) + 127
    byte = np.clip(np.where(amax > 0, byte, 1), 1, 254)
    scaled = (w * np.exp2(127.0 - byte)[:, None, :]).reshape(k, n).astype(np.float32)
    by_word = np.ascontiguousarray(scaled.reshape(k // 512, 128, 4, n).transpose(0, 1, 3, 2))
    if fmt == "e4m3":
        words = by_word.astype(ml_dtypes.float8_e4m3fn).view(np.uint8)
    else:
        c = by_word.astype(ml_dtypes.float4_e2m1fn).view(np.uint8) & 0xF
        words = (c[..., 0::2] | (c[..., 1::2] << 4)).reshape(k // 512, 128, 2 * n)
    return np.ascontiguousarray(words), np.ascontiguousarray(byte.astype(np.uint8).reshape(k // 512, 16, n))


def unpack_weight(words, scales, fmt):
    g, _, n = scales.shape
    words = np.ascontiguousarray(words).reshape(g, 128, n, -1)
    if fmt == "e4m3":
        vals = words.view(ml_dtypes.float8_e4m3fn).astype(np.float64)
    else:
        nib = np.empty((g, 128, n, 4), np.uint8)
        nib[..., 0::2] = words & 0xF
        nib[..., 1::2] = words >> 4
        vals = E2M1[nib]
    vals = vals * np.repeat(np.exp2(scales.astype(np.float64) - 127.0), 8, axis=1)[..., None]
    return vals.transpose(0, 1, 3, 2).reshape(g * 512, n)


def gelu(v):
    return 0.5 * v * (1.0 + np.tanh(np.sqrt(2.0 / np.pi) * (v + 0.044715 * v**3)))


def bf(x):
    return np.asarray(x, np.float32).astype(ml_dtypes.bfloat16)


def planes(Y):
    n, m = Y.shape
    b = f64(bf(Y)).reshape(n // 32, 32, m)
    amax = np.abs(b).max(1)
    byte = np.clip(np.where(amax > 0, np.frexp(amax)[1] - 1 + 127 - 7, 1), 1, 254)
    codes = (b * np.exp2(127.0 - byte)[:, None, :]).reshape(n, m).astype(np.float32).astype(ml_dtypes.float8_e4m3fn).view(np.uint8)
    words = codes.reshape(n // 512, 128, 4, m).transpose(0, 1, 3, 2)
    return np.ascontiguousarray(words), np.ascontiguousarray(byte.astype(np.uint8).reshape(n // 512, 16, m))


K, T, S, T2, H, N = 1024, 4096, 1024, 2048, 512, 768


def setup_inputs():
    n = np.random.standard_normal
    s = mx_kscale(K)[:, None]
    u = mx_kscale(H)[:, None]
    tab_words, tab_scales = pack_weight(n((K, T)) * s, "e4m3")
    w2_words, w2_scales = pack_weight(n((K, H)) / np.sqrt(K) / s, "e2m1")
    w3_words, w3_scales = pack_weight(n((H, N)) / np.sqrt(H) / u, "e4m3")
    return {
        "tab_words": tab_words, "tab_scales": tab_scales,
        "offs": striped(np.random.permutation(T)[:S]),
        "offs2": striped(np.random.permutation(T2)[:S]),
        "w1": (2.0 * n((K, H)) / np.sqrt(K) / s * u.T).astype(np.float32),
        "w2_words": w2_words, "w2_scales": w2_scales,
        "wgs": np.exp(0.3 * n((128, S))).astype(np.float32),
        "page0": (n((H, T2)) * u).astype(np.float32),
        "w3_words": w3_words, "w3_scales": w3_scales,
        "b3": (0.5 * n(N)).astype(np.float32),
    }


def reference(tab_words, tab_scales, offs, offs2, w1, w2_words, w2_scales, wgs, page0, w3_words, w3_scales, b3):
    v = unpack_weight(tab_words, tab_scales, "e4m3")[:, unstriped(offs)]
    a = mxq(f64(w1), 0, "e4m3").T @ v
    b = unpack_weight(w2_words, w2_scales, "e2m1").T @ v
    h = a / (1.0 + np.abs(b))
    page = f64(page0).copy()
    page[:, unstriped(offs2)] = np.tile(f64(wgs), (H // 128, 1)) * h
    c = unpack_weight(w3_words, w3_scales, "e4m3").T @ mxq(page, 0, "e4m3")
    y = np.tanh(c + f64(b3)[:, None])
    words, scales = planes(page)
    return y, page, words, scales

@@ -1,0 +1,218 @@
+from contextlib import ExitStack
+
+import concourse.mybir as mybir
+
+K, T, S, T2, H, N = 1024, 4096, 1024, 2048, 512, 768
+FLOPS = 2 * 2 * K * H * S + 2 * H * N * T2
+
+F32 = mybir.dt.float32
+BF16 = mybir.dt.bfloat16
+I32 = mybir.dt.int32
+U32 = mybir.dt.uint32
+U16 = mybir.dt.uint16
+U8 = mybir.dt.uint8
+FP8X4 = mybir.dt.float8_e4m3fn_x4
+FP4X4 = mybir.dt.float4_e2m1fn_x4
+ACT = mybir.ActivationFunctionType
+MULT = mybir.AluOpType.mult
+
+P = 128
+PACK = 4
+PASSES = K // (P * PACK)
+QUADS = 4
+BANK = 512
+HALVES = S // BANK
+N_TILES = N // P
+
+
+def tile_list_rehab_embedding_refresh_kernel(
+    tc, tab_words, tab_scales, offs, offs2, w1, w2_words, w2_scales, wgs, page0,
+    w3_words, w3_scales, b3, out_0, out_1, out_2, out_3,
+):
+    nc = tc.nc
+    with ExitStack() as ctx:
+        keep = ctx.enter_context(tc.tile_pool(name="keep", bufs=1))
+        ring = ctx.enter_context(tc.tile_pool(name="ring", bufs=2))
+        psum = ctx.enter_context(tc.psum_pool(name="psum", bufs=8))
+
+        def held(shape, dtype, name):
+            return keep.tile(shape, dtype, name=name, align_bytes=64)
+
+        picks = keep.tile([P, S // 16], U16, name="picks")
+        places = keep.tile([P, S // 16], U16, name="places")
+        nc.sync.dma_start(picks[:], offs)
+
+        tab_scale = held([P, PASSES, T], U8, "tab_scale")
+        nc.vector.memset(tab_scale[:, 0, :].bitcast(I32), 0)
+        nc.gpsimd.memset(tab_scale[:, 1, :].bitcast(I32), 0)
+        tab_scale_rows = tab_scales.bitcast(I32).rearrange("a (Q r) c -> r Q a c", r=4)
+        w2_scale_raw = held([P, PASSES, H], U8, "w2_scale_raw")
+        nc.vector.memset(w2_scale_raw[:].rearrange("p a c -> p (a c)").bitcast(I32), 0)
+        w2_scale_rows = w2_scales.bitcast(I32).rearrange("a (Q r) c -> r Q a c", r=4)
+        v_scale = held([P, PASSES, S], U8, "v_scale")
+        w3_scale = held([P, N], U8, "w3_scale")
+        nc.vector.memset(w3_scale[:].bitcast(I32), 0)
+
+        w2_raw = held([P, PASSES, 2 * H], U8, "w2_raw")
+        nc.sync.dma_start(out=w2_raw[:].bitcast(I32), in_=w2_words.bitcast(I32).rearrange("a p c -> p a c"))
+        tab = [held([P, T], U32, f"tab{a}") for a in range(PASSES)]
+        for a in range(PASSES):
+            nc.sync.dma_start(
+                out=tab[a][:].bitcast(I32),
+                in_=tab_words[a].rearrange("p t i -> p (t i)").bitcast(I32),
+            )
+            if a == 0:
+                for r in range(4):
+                    nc.sync.dma_start(out=tab_scale[r:P:32, :, :].bitcast(I32), in_=tab_scale_rows[r])
+                for r in range(4):
+                    nc.sync.dma_start(out=w2_scale_raw[r:P:32, :, :].bitcast(I32), in_=w2_scale_rows[r])
+        w1_raw = [held([P, PACK, H], F32, f"w1_raw{a}") for a in range(PASSES)]
+        w1_rows = w1.rearrange("(a p j) c -> a p j c", a=PASSES, j=PACK)
+        for a in range(PASSES):
+            nc.sync.dma_start(out=w1_raw[a][:], in_=w1_rows[a])
+        gain = [held([P, S], F32, f"gain{t}") for t in range(PACK)]
+        page = [held([P, T2], F32, f"page{t}") for t in range(PACK)]
+        gain_rows = wgs.rearrange("(q t) j -> t q j", t=PACK)
+        page_rows = page0.rearrange("(p t) c -> t p c", t=PACK)
+        for t in range(PACK):
+            for quad in (0, 2, 1, 3):
+                nc.sync.dma_start(out=gain[t][32 * quad:32 * quad + 32, :], in_=gain_rows[t])
+            if t == 0:
+                nc.sync.dma_start(places[:], offs2)
+            nc.sync.dma_start(out=page[t][:], in_=page_rows[t])
+        w3 = held([P, N], U32, "w3")
+        nc.sync.dma_start(
+            out=w3[:].bitcast(I32), in_=w3_words[0].rearrange("p c i -> p (c i)").bitcast(I32)
+        )
+        w3_scale_rows = w3_scales[0].bitcast(I32).rearrange("(Q r) c -> r Q c", r=4)
+        for r in range(4):
+            nc.sync.dma_start(out=w3_scale[r:P:32, :].bitcast(I32), in_=w3_scale_rows[r])
+        bias = held([P, N_TILES], F32, "bias")
+        with nc.allow_non_contiguous_dma(reason="one bias value to a partition"):
+            nc.sync.dma_start(out=bias[:], in_=b3.rearrange("(i p) -> p i", p=P))
+
+        w2 = held([P, PASSES, 2 * H], U8, "w2")
+        nc.vector.tensor_copy(
+            out=w2[:].rearrange("p a (t m b) -> p a t m b", t=PACK, b=2),
+            in_=w2_raw[:].rearrange("p a (m t b) -> p a t m b", t=PACK, b=2),
+        )
+        w2_scale = held([P, PASSES, H], U8, "w2_scale")
+        nc.vector.tensor_copy(
+            out=w2_scale[:].rearrange("p a (t m) -> p a t m", t=PACK),
+            in_=w2_scale_raw[:].rearrange("p a (m t) -> p a t m", t=PACK),
+        )
+
+        cols = BANK // 16
+        v = [[held([P, BANK], U32, f"v{a}_{h}") for h in range(HALVES)] for a in range(PASSES)]
+        for a in range(PASSES):
+            for h in range(HALVES):
+                nc.vector.tensor_copy(
+                    out=v[a][h][:], in_=tab[a][:].indirect(picks[:, h * cols:(h + 1) * cols])
+                )
+            if a == 0:
+                for b in range(PASSES):
+                    nc.vector.tensor_copy(out=v_scale[:, b, :], in_=tab_scale[:, b, :].indirect(picks[:]))
+
+        w1_codes = held([P, PASSES, H], U32, "w1_codes")
+        w1_scale = held([P, PASSES, H], U8, "w1_scale")
+        for a in range(PASSES):
+            grouped = held([P, H * PACK], BF16, f"w1_grouped{a}")
+            dst = grouped[:].rearrange("p (t m j) -> p m j t", t=PACK, j=PACK)
+            src = w1_raw[a][:].rearrange("p j (m t) -> p m j t", t=PACK)
+            if a == 0:
+                nc.scalar.copy(out=dst, in_=src)
+                parts = ((0, H),)
+            else:
+                nc.vector.tensor_copy(out=dst, in_=src)
+                parts = ((0, P), (P, 2 * P), (2 * P, H))
+            for c0, c1 in parts:
+                nc.vector.quantize_mx(
+                    out=w1_codes[:, a, c0:c1].bitcast(FP8X4),
+                    scales=w1_scale[:, a, c0:c1],
+                    in_=grouped[:, PACK * c0:PACK * c1],
+                )
+
+        rounded = held([P, PACK, T2], BF16, "rounded")
+        out_rows = out_1.rearrange("(p t) c -> t p c", t=PACK)
+        for t in range(PACK):
+            rows = slice(t * P, (t + 1) * P)
+            for h in range(HALVES):
+                picked = slice(h * BANK, (h + 1) * BANK)
+                acc_b = psum.tile([P, BANK], F32, name="acc")
+                for a in range(PASSES):
+                    nc.tensor.matmul_mx(
+                        out=acc_b[:],
+                        lhsT=w2[:, a, 2 * t * P:2 * (t + 1) * P].bitcast(FP4X4),
+                        lhsT_scale=w2_scale[:, a, rows],
+                        rhs=v[a][h][:].bitcast(FP8X4),
+                        rhs_scale=v_scale[:, a, picked],
+                        start=(a == 0),
+                        stop=(a == PASSES - 1),
+                    )
+                acc_a = psum.tile([P, BANK], F32, name="acc")
+                for a in range(PASSES):
+                    nc.tensor.matmul_mx(
+                        out=acc_a[:],
+                        lhsT=w1_codes[:, a, rows].bitcast(FP8X4),
+                        lhsT_scale=w1_scale[:, a, rows],
+                        rhs=v[a][h][:].bitcast(FP8X4),
+                        rhs_scale=v_scale[:, a, picked],
+                        start=(a == 0),
+                        stop=(a == PASSES - 1),
+                    )
+                size = w1_raw[0][:, (HALVES * t + h) % PACK, :]
+                nc.scalar.activation(out=size, in_=acc_b[:], func=ACT.Abs)
+                root = ring.tile([P, BANK], F32, name="root")
+                nc.scalar.activation(out=root[:], in_=size, func=ACT.Abs_reciprocal_sqrt, bias=1.0)
+                damp = ring.tile([P, BANK], F32, name="damp", bufs=6)
+                nc.scalar.activation(out=damp[:], in_=root[:], func=ACT.Square)
+                hidden = ring.tile([P, BANK], F32, name="hidden", bufs=3)
+                nc.vector.tensor_tensor(out=hidden[:], in0=acc_a[:], in1=damp[:], op=MULT)
+                nc.vector.tensor_tensor(
+                    out=page[t][:].indirect(places[:, h * cols:(h + 1) * cols]),
+                    in0=hidden[:],
+                    in1=gain[t][:, picked],
+                    op=MULT,
+                )
+            nc.sync.dma_start(out=out_rows[t], in_=page[t][:])
+        for t in range(PACK - 1):
+            nc.scalar.copy(out=rounded[:, t, :], in_=page[t][:])
+
+        codes = held([P, T2], U32, "codes")
+        scale = held([P, T2], U8, "scale")
+        code_rows = out_2[0].rearrange("p c i -> p (c i)").bitcast(I32)
+        for c0 in range(0, T2, BANK):
+            chunk = slice(c0, c0 + BANK)
+            nc.vector.tensor_copy(out=rounded[:, PACK - 1, chunk], in_=page[PACK - 1][:, chunk])
+            woven = ring.tile([P, BANK, PACK], BF16, name="woven", align_bytes=64)
+            nc.vector.tensor_copy(
+                out=woven[:].rearrange("p (c i) t -> p c t i", i=4),
+                in_=rounded[:, :, chunk].rearrange("p t (c i) -> p c t i", i=4),
+            )
+            nc.vector.quantize_mx(
+                out=codes[:, chunk].bitcast(FP8X4),
+                scales=scale[:, chunk],
+                in_=woven[:].rearrange("p c t -> p (c t)"),
+            )
+            nc.sync.dma_start(out=code_rows[:, chunk], in_=codes[:, chunk].bitcast(I32))
+            for i in range(N_TILES):
+                rows = slice(i * P, (i + 1) * P)
+                acc_c = psum.tile([P, BANK], F32, name="acc")
+                nc.tensor.matmul_mx(
+                    out=acc_c[:],
+                    lhsT=w3[:, rows].bitcast(FP8X4),
+                    lhsT_scale=w3_scale[:, rows],
+                    rhs=codes[:, chunk].bitcast(FP8X4),
+                    rhs_scale=scale[:, chunk],
+                    start=True,
+                    stop=True,
+                )
+                y = ring.tile([P, BANK], F32, name="y", bufs=10)
+                nc.scalar.activation(out=y[:], in_=acc_c[:], func=ACT.Tanh, bias=bias[:, i:i + 1])
+                nc.sync.dma_start(out=out_0[rows, chunk], in_=y[:])
+        scale_rows = out_3[0].bitcast(I32)
+        for quad in range(QUADS):
+            nc.gpsimd.dma_start(
+                out=scale_rows[4 * quad:4 * quad + 4, :],
+                in_=scale[32 * quad:32 * quad + 4, :].bitcast(I32),
+            )

@@ -33,14 +33,18 @@ def tile_list_rehab_embedding_refresh_kernel(
     with ExitStack() as ctx:
         keep = ctx.enter_context(tc.tile_pool(name="keep", bufs=1))
         ring = ctx.enter_context(tc.tile_pool(name="ring", bufs=2))
-        psum = ctx.enter_context(tc.psum_pool(name="psum", bufs=8))
+        psum = ctx.enter_context(tc.psum_pool(name="psum", bufs=1))
 
         def held(shape, dtype, name):
-            return keep.tile(shape, dtype, name=name, align_bytes=64)
+            return keep.tile(shape, dtype, name=name, tag=name, align_bytes=64)
 
         picks = keep.tile([P, S // 16], U16, name="picks")
         places = keep.tile([P, S // 16], U16, name="places")
         nc.sync.dma_start(picks[:], offs)
+
+        warm = held([P, 3], F32, "warm")
+        nc.vector.memset(warm[:, 0:1], 1.0)
+        nc.scalar.activation(out=warm[:, 1:2], in_=warm[:, 0:1], func=ACT.Abs_reciprocal_sqrt)
 
         tab_scale = held([P, PASSES, T], U8, "tab_scale")
         nc.vector.memset(tab_scale[:, 0, :].bitcast(I32), 0)
@@ -55,6 +59,8 @@ def tile_list_rehab_embedding_refresh_kernel(
 
         w2_raw = held([P, PASSES, 2 * H], U8, "w2_raw")
         nc.sync.dma_start(out=w2_raw[:].bitcast(I32), in_=w2_words.bitcast(I32).rearrange("a p c -> p a c"))
+        w1_raw = [held([P, PACK, H], F32, f"w1_raw{a}") for a in range(PASSES)]
+        w1_rows = w1.rearrange("(a p j) c -> a p j c", a=PASSES, j=PACK)
         tab = [held([P, T], U32, f"tab{a}") for a in range(PASSES)]
         for a in range(PASSES):
             nc.sync.dma_start(
@@ -66,20 +72,21 @@ def tile_list_rehab_embedding_refresh_kernel(
                     nc.sync.dma_start(out=tab_scale[r:P:32, :, :].bitcast(I32), in_=tab_scale_rows[r])
                 for r in range(4):
                     nc.sync.dma_start(out=w2_scale_raw[r:P:32, :, :].bitcast(I32), in_=w2_scale_rows[r])
-        w1_raw = [held([P, PACK, H], F32, f"w1_raw{a}") for a in range(PASSES)]
-        w1_rows = w1.rearrange("(a p j) c -> a p j c", a=PASSES, j=PACK)
-        for a in range(PASSES):
             nc.sync.dma_start(out=w1_raw[a][:], in_=w1_rows[a])
         gain = [held([P, S], F32, f"gain{t}") for t in range(PACK)]
         page = [held([P, T2], F32, f"page{t}") for t in range(PACK)]
         gain_rows = wgs.rearrange("(q t) j -> t q j", t=PACK)
         page_rows = page0.rearrange("(p t) c -> t p c", t=PACK)
         for t in range(PACK):
+            early = BANK if t == 0 else S
             for quad in (0, 2, 1, 3):
-                nc.sync.dma_start(out=gain[t][32 * quad:32 * quad + 32, :], in_=gain_rows[t])
+                nc.sync.dma_start(out=gain[t][32 * quad:32 * quad + 32, :early], in_=gain_rows[t][:, :early])
             if t == 0:
                 nc.sync.dma_start(places[:], offs2)
             nc.sync.dma_start(out=page[t][:], in_=page_rows[t])
+            if early < S:
+                for quad in (0, 2, 1, 3):
+                    nc.sync.dma_start(out=gain[t][32 * quad:32 * quad + 32, early:], in_=gain_rows[t][:, early:])
         w3 = held([P, N], U32, "w3")
         nc.sync.dma_start(
             out=w3[:].bitcast(I32), in_=w3_words[0].rearrange("p c i -> p (c i)").bitcast(I32)
@@ -136,9 +143,10 @@ def tile_list_rehab_embedding_refresh_kernel(
         out_rows = out_1.rearrange("(p t) c -> t p c", t=PACK)
         for t in range(PACK):
             rows = slice(t * P, (t + 1) * P)
+            fresh = held([P, S], F32, f"fresh{t}")
             for h in range(HALVES):
                 picked = slice(h * BANK, (h + 1) * BANK)
-                acc_b = psum.tile([P, BANK], F32, name="acc")
+                acc_b = psum.tile([P, BANK], F32, name="acc", bufs=3)
                 for a in range(PASSES):
                     nc.tensor.matmul_mx(
                         out=acc_b[:],
@@ -149,7 +157,7 @@ def tile_list_rehab_embedding_refresh_kernel(
                         start=(a == 0),
                         stop=(a == PASSES - 1),
                     )
-                acc_a = psum.tile([P, BANK], F32, name="acc")
+                acc_a = psum.tile([P, BANK], F32, name="acc", bufs=3)
                 for a in range(PASSES):
                     nc.tensor.matmul_mx(
                         out=acc_a[:],
@@ -164,40 +172,67 @@ def tile_list_rehab_embedding_refresh_kernel(
                 nc.scalar.activation(out=size, in_=acc_b[:], func=ACT.Abs)
                 root = ring.tile([P, BANK], F32, name="root")
                 nc.scalar.activation(out=root[:], in_=size, func=ACT.Abs_reciprocal_sqrt, bias=1.0)
-                damp = ring.tile([P, BANK], F32, name="damp", bufs=6)
+                damp = ring.tile([P, BANK], F32, name="damp", bufs=4)
                 nc.scalar.activation(out=damp[:], in_=root[:], func=ACT.Square)
-                hidden = ring.tile([P, BANK], F32, name="hidden", bufs=3)
-                nc.vector.tensor_tensor(out=hidden[:], in0=acc_a[:], in1=damp[:], op=MULT)
-                nc.vector.tensor_tensor(
-                    out=page[t][:].indirect(places[:, h * cols:(h + 1) * cols]),
-                    in0=hidden[:],
-                    in1=gain[t][:, picked],
-                    op=MULT,
-                )
+                partial = ring.tile([P, BANK], F32, name="partial")
+                if t == 0 and h == 0:
+                    nc.vector.tensor_tensor(out=partial[:], in0=damp[:], in1=gain[t][:, picked], op=MULT)
+                    nc.vector.tensor_tensor(out=fresh[:, picked], in0=acc_a[:], in1=partial[:], op=MULT)
+                else:
+                    raw = ring.tile([P, BANK], F32, name="raw", bufs=3)
+                    nc.scalar.copy(out=raw[:], in_=acc_a[:])
+                    nc.gpsimd.tensor_tensor(out=partial[:], in0=raw[:], in1=damp[:], op=MULT)
+                    nc.gpsimd.tensor_tensor(out=fresh[:, picked], in0=partial[:], in1=gain[t][:, picked], op=MULT)
+                if t < 2:
+                    nc.vector.tensor_copy(
+                        out=page[t][:].indirect(places[:, h * cols:(h + 1) * cols]), in_=fresh[:, picked]
+                    )
+            if t >= 2:
+                nc.vector.tensor_copy(out=page[t][:].indirect(places[:]), in_=fresh[:])
             nc.sync.dma_start(out=out_rows[t], in_=page[t][:])
         for t in range(PACK - 1):
             nc.scalar.copy(out=rounded[:, t, :], in_=page[t][:])
+        nc.scalar.activation(out=warm[:, 2:3], in_=damp[:, 0:1], func=ACT.Tanh)
 
         codes = held([P, T2], U32, "codes")
         scale = held([P, T2], U8, "scale")
+        spare = ("tab0", "tab1", "features_a", "features_b")
+        scale_rows = out_3[0].bitcast(I32)
         code_rows = out_2[0].rearrange("p c i -> p (c i)").bitcast(I32)
         for c0 in range(0, T2, BANK):
             chunk = slice(c0, c0 + BANK)
-            nc.vector.tensor_copy(out=rounded[:, PACK - 1, chunk], in_=page[PACK - 1][:, chunk])
-            woven = ring.tile([P, BANK, PACK], BF16, name="woven", align_bytes=64)
-            nc.vector.tensor_copy(
-                out=woven[:].rearrange("p (c i) t -> p c t i", i=4),
-                in_=rounded[:, :, chunk].rearrange("p t (c i) -> p c t i", i=4),
-            )
-            nc.vector.quantize_mx(
-                out=codes[:, chunk].bitcast(FP8X4),
-                scales=scale[:, chunk],
-                in_=woven[:].rearrange("p c t -> p (c t)"),
+            woven = ring.tile([P, BANK, PACK], BF16, name="woven", bufs=1, align_bytes=64)
+            if c0 == 0:
+                shares = ((nc.vector.tensor_copy, 0, BANK // 2), (nc.scalar.copy, BANK // 2, BANK))
+            else:
+                shares = ((nc.vector.tensor_copy, 0, BANK),)
+            for move, lo, hi in shares:
+                part = slice(c0 + lo, c0 + hi)
+                move(out=rounded[:, PACK - 1, part], in_=page[PACK - 1][:, part])
+                move(
+                    out=woven[:, lo:hi, :].rearrange("p (c i) t -> p c t i", i=4),
+                    in_=rounded[:, :, part].rearrange("p t (c i) -> p c t i", i=4),
+                )
+            for move, lo, hi in shares:
+                part = slice(c0 + lo, c0 + hi)
+                nc.vector.quantize_mx(
+                    out=codes[:, part].bitcast(FP8X4),
+                    scales=scale[:, part],
+                    in_=woven[:, lo:hi, :].rearrange("p c t -> p (c t)"),
+                )
+            features = keep.tile(
+                [P, N_TILES, BANK], F32, name=f"features{c0}", tag=spare[c0 // BANK], align_bytes=64
             )
             nc.sync.dma_start(out=code_rows[:, chunk], in_=codes[:, chunk].bitcast(I32))
+            if c0 + BANK == T2:
+                for quad in range(QUADS):
+                    nc.sync.dma_start(
+                        out=scale_rows[4 * quad:4 * quad + 4, :],
+                        in_=scale[32 * quad:32 * quad + 4, :].bitcast(I32),
+                    )
             for i in range(N_TILES):
                 rows = slice(i * P, (i + 1) * P)
-                acc_c = psum.tile([P, BANK], F32, name="acc")
+                acc_c = psum.tile([P, BANK], F32, name="acc_c", bufs=5)
                 nc.tensor.matmul_mx(
                     out=acc_c[:],
                     lhsT=w3[:, rows].bitcast(FP8X4),
@@ -207,12 +242,5 @@ def tile_list_rehab_embedding_refresh_kernel(
                     start=True,
                     stop=True,
                 )
-                y = ring.tile([P, BANK], F32, name="y", bufs=10)
-                nc.scalar.activation(out=y[:], in_=acc_c[:], func=ACT.Tanh, bias=bias[:, i:i + 1])
-                nc.sync.dma_start(out=out_0[rows, chunk], in_=y[:])
-        scale_rows = out_3[0].bitcast(I32)
-        for quad in range(QUADS):
-            nc.gpsimd.dma_start(
-                out=scale_rows[4 * quad:4 * quad + 4, :],
-                in_=scale[32 * quad:32 * quad + 4, :].bitcast(I32),
-            )
+                nc.scalar.activation(out=features[:, i, :], in_=acc_c[:], func=ACT.Tanh, bias=bias[:, i:i + 1])
+                nc.sync.dma_start(out=out_0[rows, chunk], in_=features[:, i, :])

@@ -46,14 +46,19 @@ def tile_list_rehab_embedding_refresh_kernel(
         nc.vector.memset(warm[:, 0:1], 1.0)
         nc.scalar.activation(out=warm[:, 1:2], in_=warm[:, 0:1], func=ACT.Abs_reciprocal_sqrt)
 
-        tab_scale = held([P, PASSES, T], U8, "tab_scale")
-        nc.vector.memset(tab_scale[:, 0, :].bitcast(I32), 0)
-        nc.gpsimd.memset(tab_scale[:, 1, :].bitcast(I32), 0)
-        tab_scale_rows = tab_scales.bitcast(I32).rearrange("a (Q r) c -> r Q a c", r=4)
+        tab_rows = held([P, T], U8, "tab_rows")
+        nc.vector.memset(tab_rows[:].bitcast(I32), 0)
+        nc.gpsimd.dma_start(
+            out=tab_rows[0:P:4, :].bitcast(I32),
+            in_=tab_scales.rearrange("a q t -> (a q) t").bitcast(I32),
+        )
         w2_scale_raw = held([P, PASSES, H], U8, "w2_scale_raw")
         nc.vector.memset(w2_scale_raw[:].rearrange("p a c -> p (a c)").bitcast(I32), 0)
         w2_scale_rows = w2_scales.bitcast(I32).rearrange("a (Q r) c -> r Q a c", r=4)
+        for r in range(4):
+            nc.gpsimd.dma_start(out=w2_scale_raw[r:P:32, :, :].bitcast(I32), in_=w2_scale_rows[r])
         v_scale = held([P, PASSES, S], U8, "v_scale")
+        nc.vector.memset(v_scale[:].rearrange("p a c -> p (a c)").bitcast(I32), 0)
         w3_scale = held([P, N], U8, "w3_scale")
         nc.vector.memset(w3_scale[:].bitcast(I32), 0)
 
@@ -67,18 +72,13 @@ def tile_list_rehab_embedding_refresh_kernel(
                 out=tab[a][:].bitcast(I32),
                 in_=tab_words[a].rearrange("p t i -> p (t i)").bitcast(I32),
             )
-            if a == 0:
-                for r in range(4):
-                    nc.sync.dma_start(out=tab_scale[r:P:32, :, :].bitcast(I32), in_=tab_scale_rows[r])
-                for r in range(4):
-                    nc.sync.dma_start(out=w2_scale_raw[r:P:32, :, :].bitcast(I32), in_=w2_scale_rows[r])
             nc.sync.dma_start(out=w1_raw[a][:], in_=w1_rows[a])
         gain = [held([P, S], F32, f"gain{t}") for t in range(PACK)]
         page = [held([P, T2], F32, f"page{t}") for t in range(PACK)]
         gain_rows = wgs.rearrange("(q t) j -> t q j", t=PACK)
         page_rows = page0.rearrange("(p t) c -> t p c", t=PACK)
         for t in range(PACK):
-            early = BANK if t == 0 else S
+            early = BANK if t < 2 else S
             for quad in (0, 2, 1, 3):
                 nc.sync.dma_start(out=gain[t][32 * quad:32 * quad + 32, :early], in_=gain_rows[t][:, :early])
             if t == 0:
@@ -109,16 +109,28 @@ def tile_list_rehab_embedding_refresh_kernel(
             in_=w2_scale_raw[:].rearrange("p a (m t) -> p a t m", t=PACK),
         )
 
+        picked_rows = held([P, S], U8, "picked_rows")
+        nc.vector.tensor_copy(out=picked_rows[:], in_=tab_rows[:].indirect(picks[:]))
+        for a in range(PASSES):
+            for quad in range(QUADS):
+                first = 64 * a + 16 * quad
+                nc.gpsimd.dma_start(
+                    out=v_scale[32 * quad:32 * quad + 4, a, :].bitcast(I32),
+                    in_=picked_rows[first:first + 16:4, :].bitcast(I32),
+                )
         cols = BANK // 16
-        v = [[held([P, BANK], U32, f"v{a}_{h}") for h in range(HALVES)] for a in range(PASSES)]
+        v = [
+            [
+                keep.tile([P, BANK], U32, name=f"v{a}_{h}", tag="tab_rows" if a + h == 0 else f"v{a}_{h}", align_bytes=64)
+                for h in range(HALVES)
+            ]
+            for a in range(PASSES)
+        ]
         for a in range(PASSES):
             for h in range(HALVES):
                 nc.vector.tensor_copy(
                     out=v[a][h][:], in_=tab[a][:].indirect(picks[:, h * cols:(h + 1) * cols])
                 )
-            if a == 0:
-                for b in range(PASSES):
-                    nc.vector.tensor_copy(out=v_scale[:, b, :], in_=tab_scale[:, b, :].indirect(picks[:]))
 
         w1_codes = held([P, PASSES, H], U32, "w1_codes")
         w1_scale = held([P, PASSES, H], U8, "w1_scale")
@@ -141,39 +153,37 @@ def tile_list_rehab_embedding_refresh_kernel(
 
         rounded = held([P, PACK, T2], BF16, "rounded")
         out_rows = out_1.rearrange("(p t) c -> t p c", t=PACK)
+        def product(words, scales, dtype, width, t, h):
+            acc = psum.tile([P, BANK], F32, name="acc", bufs=3)
+            for a in range(PASSES):
+                nc.tensor.matmul_mx(
+                    out=acc[:],
+                    lhsT=words[:, a, width * t * P:width * (t + 1) * P].bitcast(dtype),
+                    lhsT_scale=scales[:, a, t * P:(t + 1) * P],
+                    rhs=v[a][h][:].bitcast(FP8X4),
+                    rhs_scale=v_scale[:, a, h * BANK:(h + 1) * BANK],
+                    start=(a == 0),
+                    stop=(a == PASSES - 1),
+                )
+            return acc
+
+        def damping(t, h):
+            acc_b = product(w2, w2_scale, FP4X4, 2, t, h)
+            size = w1_raw[0][:, (HALVES * t + h) % PACK, :]
+            nc.scalar.activation(out=size, in_=acc_b[:], func=ACT.Abs)
+            root = ring.tile([P, BANK], F32, name="root")
+            nc.scalar.activation(out=root[:], in_=size, func=ACT.Abs_reciprocal_sqrt, bias=1.0)
+            damp = ring.tile([P, BANK], F32, name="damp", bufs=4)
+            nc.scalar.activation(out=damp[:], in_=root[:], func=ACT.Square)
+            return damp
+
+        first_damps = [damping(0, h) for h in range(HALVES)]
         for t in range(PACK):
-            rows = slice(t * P, (t + 1) * P)
             fresh = held([P, S], F32, f"fresh{t}")
             for h in range(HALVES):
                 picked = slice(h * BANK, (h + 1) * BANK)
-                acc_b = psum.tile([P, BANK], F32, name="acc", bufs=3)
-                for a in range(PASSES):
-                    nc.tensor.matmul_mx(
-                        out=acc_b[:],
-                        lhsT=w2[:, a, 2 * t * P:2 * (t + 1) * P].bitcast(FP4X4),
-                        lhsT_scale=w2_scale[:, a, rows],
-                        rhs=v[a][h][:].bitcast(FP8X4),
-                        rhs_scale=v_scale[:, a, picked],
-                        start=(a == 0),
-                        stop=(a == PASSES - 1),
-                    )
-                acc_a = psum.tile([P, BANK], F32, name="acc", bufs=3)
-                for a in range(PASSES):
-                    nc.tensor.matmul_mx(
-                        out=acc_a[:],
-                        lhsT=w1_codes[:, a, rows].bitcast(FP8X4),
-                        lhsT_scale=w1_scale[:, a, rows],
-                        rhs=v[a][h][:].bitcast(FP8X4),
-                        rhs_scale=v_scale[:, a, picked],
-                        start=(a == 0),
-                        stop=(a == PASSES - 1),
-                    )
-                size = w1_raw[0][:, (HALVES * t + h) % PACK, :]
-                nc.scalar.activation(out=size, in_=acc_b[:], func=ACT.Abs)
-                root = ring.tile([P, BANK], F32, name="root")
-                nc.scalar.activation(out=root[:], in_=size, func=ACT.Abs_reciprocal_sqrt, bias=1.0)
-                damp = ring.tile([P, BANK], F32, name="damp", bufs=4)
-                nc.scalar.activation(out=damp[:], in_=root[:], func=ACT.Square)
+                damp = first_damps[h] if t == 0 else damping(t, h)
+                acc_a = product(w1_codes, w1_scale, FP8X4, 1, t, h)
                 partial = ring.tile([P, BANK], F32, name="partial")
                 if t == 0 and h == 0:
                     nc.vector.tensor_tensor(out=partial[:], in0=damp[:], in1=gain[t][:, picked], op=MULT)
@@ -196,11 +206,10 @@ def tile_list_rehab_embedding_refresh_kernel(
 
         codes = held([P, T2], U32, "codes")
         scale = held([P, T2], U8, "scale")
-        spare = ("tab0", "tab1", "features_a", "features_b")
         scale_rows = out_3[0].bitcast(I32)
         code_rows = out_2[0].rearrange("p c i -> p (c i)").bitcast(I32)
-        for c0 in range(0, T2, BANK):
-            chunk = slice(c0, c0 + BANK)
+
+        def quantise(c0):
             woven = ring.tile([P, BANK, PACK], BF16, name="woven", bufs=1, align_bytes=64)
             if c0 == 0:
                 shares = ((nc.vector.tensor_copy, 0, BANK // 2), (nc.scalar.copy, BANK // 2, BANK))
@@ -220,27 +229,33 @@ def tile_list_rehab_embedding_refresh_kernel(
                     scales=scale[:, part],
                     in_=woven[:, lo:hi, :].rearrange("p c t -> p (c t)"),
                 )
-            features = keep.tile(
-                [P, N_TILES, BANK], F32, name=f"features{c0}", tag=spare[c0 // BANK], align_bytes=64
-            )
-            nc.sync.dma_start(out=code_rows[:, chunk], in_=codes[:, chunk].bitcast(I32))
-            if c0 + BANK == T2:
+
+        for s0, s1, space in ((0, BANK, "features"), (BANK, 2 * BANK, "tab1"), (2 * BANK, T2, "tab0")):
+            for c0 in range(s0, s1, BANK):
+                quantise(c0)
+            nc.sync.dma_start(out=code_rows[:, s0:s1], in_=codes[:, s0:s1].bitcast(I32))
+            if s1 == T2:
                 for quad in range(QUADS):
                     nc.sync.dma_start(
                         out=scale_rows[4 * quad:4 * quad + 4, :],
                         in_=scale[32 * quad:32 * quad + 4, :].bitcast(I32),
                     )
+            features = keep.tile([P, N_TILES, s1 - s0], F32, name=f"features{s0}", tag=space, align_bytes=64)
             for i in range(N_TILES):
                 rows = slice(i * P, (i + 1) * P)
-                acc_c = psum.tile([P, BANK], F32, name="acc_c", bufs=5)
-                nc.tensor.matmul_mx(
-                    out=acc_c[:],
-                    lhsT=w3[:, rows].bitcast(FP8X4),
-                    lhsT_scale=w3_scale[:, rows],
-                    rhs=codes[:, chunk].bitcast(FP8X4),
-                    rhs_scale=scale[:, chunk],
-                    start=True,
-                    stop=True,
-                )
-                nc.scalar.activation(out=features[:, i, :], in_=acc_c[:], func=ACT.Tanh, bias=bias[:, i:i + 1])
-                nc.sync.dma_start(out=out_0[rows, chunk], in_=features[:, i, :])
+                for c0 in range(s0, s1, BANK):
+                    chunk = slice(c0, c0 + BANK)
+                    acc_c = psum.tile([P, BANK], F32, name="acc_c", bufs=5)
+                    nc.tensor.matmul_mx(
+                        out=acc_c[:],
+                        lhsT=w3[:, rows].bitcast(FP8X4),
+                        lhsT_scale=w3_scale[:, rows],
+                        rhs=codes[:, chunk].bitcast(FP8X4),
+                        rhs_scale=scale[:, chunk],
+                        start=True,
+                        stop=True,
+                    )
+                    nc.scalar.activation(
+                        out=features[:, i, c0 - s0:c0 - s0 + BANK], in_=acc_c[:], func=ACT.Tanh, bias=bias[:, i:i + 1]
+                    )
+                nc.sync.dma_start(out=out_0[rows, s0:s1], in_=features[:, i, :])

@@ -42,21 +42,16 @@ def tile_list_rehab_embedding_refresh_kernel(
         places = keep.tile([P, S // 16], U16, name="places")
         nc.sync.dma_start(picks[:], offs)
 
+        w2_scale_raw = held([P, PASSES, H], U8, "w2_scale_raw")
+        nc.gpsimd.memset(w2_scale_raw[:].rearrange("p a c -> p (a c)").bitcast(I32), 0)
+        tab_rows = held([P, T], U8, "tab_rows")
+        nc.vector.memset(tab_rows[:, :T // 2].bitcast(I32), 0)
+        nc.gpsimd.memset(tab_rows[:, T // 2:].bitcast(I32), 0)
         warm = held([P, 3], F32, "warm")
         nc.vector.memset(warm[:, 0:1], 1.0)
         nc.scalar.activation(out=warm[:, 1:2], in_=warm[:, 0:1], func=ACT.Abs_reciprocal_sqrt)
 
-        tab_rows = held([P, T], U8, "tab_rows")
-        nc.vector.memset(tab_rows[:].bitcast(I32), 0)
-        nc.gpsimd.dma_start(
-            out=tab_rows[0:P:4, :].bitcast(I32),
-            in_=tab_scales.rearrange("a q t -> (a q) t").bitcast(I32),
-        )
-        w2_scale_raw = held([P, PASSES, H], U8, "w2_scale_raw")
-        nc.vector.memset(w2_scale_raw[:].rearrange("p a c -> p (a c)").bitcast(I32), 0)
         w2_scale_rows = w2_scales.bitcast(I32).rearrange("a (Q r) c -> r Q a c", r=4)
-        for r in range(4):
-            nc.gpsimd.dma_start(out=w2_scale_raw[r:P:32, :, :].bitcast(I32), in_=w2_scale_rows[r])
         v_scale = held([P, PASSES, S], U8, "v_scale")
         nc.vector.memset(v_scale[:].rearrange("p a c -> p (a c)").bitcast(I32), 0)
         w3_scale = held([P, N], U8, "w3_scale")
@@ -64,6 +59,12 @@ def tile_list_rehab_embedding_refresh_kernel(
 
         w2_raw = held([P, PASSES, 2 * H], U8, "w2_raw")
         nc.sync.dma_start(out=w2_raw[:].bitcast(I32), in_=w2_words.bitcast(I32).rearrange("a p c -> p a c"))
+        for r in range(4):
+            nc.sync.dma_start(out=w2_scale_raw[r:P:32, :, :].bitcast(I32), in_=w2_scale_rows[r])
+        nc.sync.dma_start(
+            out=tab_rows[0:P:4, :].bitcast(I32),
+            in_=tab_scales.rearrange("a q t -> (a q) t").bitcast(I32),
+        )
         w1_raw = [held([P, PACK, H], F32, f"w1_raw{a}") for a in range(PASSES)]
         w1_rows = w1.rearrange("(a p j) c -> a p j c", a=PASSES, j=PACK)
         tab = [held([P, T], U32, f"tab{a}") for a in range(PASSES)]
@@ -119,13 +120,7 @@ def tile_list_rehab_embedding_refresh_kernel(
                     in_=picked_rows[first:first + 16:4, :].bitcast(I32),
                 )
         cols = BANK // 16
-        v = [
-            [
-                keep.tile([P, BANK], U32, name=f"v{a}_{h}", tag="tab_rows" if a + h == 0 else f"v{a}_{h}", align_bytes=64)
-                for h in range(HALVES)
-            ]
-            for a in range(PASSES)
-        ]
+        v = [[held([P, BANK], U32, f"v{a}_{h}") for h in range(HALVES)] for a in range(PASSES)]
         for a in range(PASSES):
             for h in range(HALVES):
                 nc.vector.tensor_copy(

@@ -42,29 +42,27 @@ def tile_list_rehab_embedding_refresh_kernel(
         places = keep.tile([P, S // 16], U16, name="places")
         nc.sync.dma_start(picks[:], offs)
 
-        w2_scale_raw = held([P, PASSES, H], U8, "w2_scale_raw")
-        nc.gpsimd.memset(w2_scale_raw[:].rearrange("p a c -> p (a c)").bitcast(I32), 0)
         tab_rows = held([P, T], U8, "tab_rows")
         nc.vector.memset(tab_rows[:, :T // 2].bitcast(I32), 0)
         nc.gpsimd.memset(tab_rows[:, T // 2:].bitcast(I32), 0)
+        w2_scale_raw = held([P, PASSES, H], U8, "w2_scale_raw")
+        nc.gpsimd.memset(w2_scale_raw[:].rearrange("p a c -> p (a c)").bitcast(I32), 0)
         warm = held([P, 3], F32, "warm")
         nc.vector.memset(warm[:, 0:1], 1.0)
         nc.scalar.activation(out=warm[:, 1:2], in_=warm[:, 0:1], func=ACT.Abs_reciprocal_sqrt)
 
         w2_scale_rows = w2_scales.bitcast(I32).rearrange("a (Q r) c -> r Q a c", r=4)
-        v_scale = held([P, PASSES, S], U8, "v_scale")
-        nc.vector.memset(v_scale[:].rearrange("p a c -> p (a c)").bitcast(I32), 0)
+        second_rows = held([P, S], U8, "second_rows")
+        nc.vector.memset(second_rows[:].bitcast(I32), 0)
         w3_scale = held([P, N], U8, "w3_scale")
         nc.vector.memset(w3_scale[:].bitcast(I32), 0)
 
         w2_raw = held([P, PASSES, 2 * H], U8, "w2_raw")
         nc.sync.dma_start(out=w2_raw[:].bitcast(I32), in_=w2_words.bitcast(I32).rearrange("a p c -> p a c"))
+        nc.sync.dma_start(out=tab_rows[4:P:8, :].bitcast(I32), in_=tab_scales[1].bitcast(I32))
+        first_rows = tab_scales[0].bitcast(I32).rearrange("(Q r) c -> r Q c", r=4)
         for r in range(4):
-            nc.sync.dma_start(out=w2_scale_raw[r:P:32, :, :].bitcast(I32), in_=w2_scale_rows[r])
-        nc.sync.dma_start(
-            out=tab_rows[0:P:4, :].bitcast(I32),
-            in_=tab_scales.rearrange("a q t -> (a q) t").bitcast(I32),
-        )
+            nc.sync.dma_start(out=tab_rows[r:P:32, :].bitcast(I32), in_=first_rows[r])
         w1_raw = [held([P, PACK, H], F32, f"w1_raw{a}") for a in range(PASSES)]
         w1_rows = w1.rearrange("(a p j) c -> a p j c", a=PASSES, j=PACK)
         tab = [held([P, T], U32, f"tab{a}") for a in range(PASSES)]
@@ -73,6 +71,9 @@ def tile_list_rehab_embedding_refresh_kernel(
                 out=tab[a][:].bitcast(I32),
                 in_=tab_words[a].rearrange("p t i -> p (t i)").bitcast(I32),
             )
+            if a == 0:
+                for r in range(4):
+                    nc.sync.dma_start(out=w2_scale_raw[r:P:32, :, :].bitcast(I32), in_=w2_scale_rows[r])
             nc.sync.dma_start(out=w1_raw[a][:], in_=w1_rows[a])
         gain = [held([P, S], F32, f"gain{t}") for t in range(PACK)]
         page = [held([P, T2], F32, f"page{t}") for t in range(PACK)]
@@ -99,6 +100,13 @@ def tile_list_rehab_embedding_refresh_kernel(
         with nc.allow_non_contiguous_dma(reason="one bias value to a partition"):
             nc.sync.dma_start(out=bias[:], in_=b3.rearrange("(i p) -> p i", p=P))
 
+        picked_rows = held([P, S], U8, "picked_rows")
+        nc.vector.tensor_copy(out=picked_rows[:], in_=tab_rows[:].indirect(picks[:]))
+        for r in range(4):
+            nc.gpsimd.dma_start(
+                out=second_rows[r:P:32, :].bitcast(I32), in_=picked_rows[8 * r + 4:P:32, :].bitcast(I32)
+            )
+        v_scale = (picked_rows, second_rows)
         w2 = held([P, PASSES, 2 * H], U8, "w2")
         nc.vector.tensor_copy(
             out=w2[:].rearrange("p a (t m b) -> p a t m b", t=PACK, b=2),
@@ -110,15 +118,6 @@ def tile_list_rehab_embedding_refresh_kernel(
             in_=w2_scale_raw[:].rearrange("p a (m t) -> p a t m", t=PACK),
         )
 
-        picked_rows = held([P, S], U8, "picked_rows")
-        nc.vector.tensor_copy(out=picked_rows[:], in_=tab_rows[:].indirect(picks[:]))
-        for a in range(PASSES):
-            for quad in range(QUADS):
-                first = 64 * a + 16 * quad
-                nc.gpsimd.dma_start(
-                    out=v_scale[32 * quad:32 * quad + 4, a, :].bitcast(I32),
-                    in_=picked_rows[first:first + 16:4, :].bitcast(I32),
-                )
         cols = BANK // 16
         v = [[held([P, BANK], U32, f"v{a}_{h}") for h in range(HALVES)] for a in range(PASSES)]
         for a in range(PASSES):
@@ -156,7 +155,7 @@ def tile_list_rehab_embedding_refresh_kernel(
                     lhsT=words[:, a, width * t * P:width * (t + 1) * P].bitcast(dtype),
                     lhsT_scale=scales[:, a, t * P:(t + 1) * P],
                     rhs=v[a][h][:].bitcast(FP8X4),
-                    rhs_scale=v_scale[:, a, h * BANK:(h + 1) * BANK],
+                    rhs_scale=v_scale[a][:, h * BANK:(h + 1) * BANK],
                     start=(a == 0),
                     stop=(a == PASSES - 1),
                 )

@@ -43,52 +43,74 @@ def tile_list_rehab_embedding_refresh_kernel(
         nc.sync.dma_start(picks[:], offs)
 
         tab_rows = held([P, T], U8, "tab_rows")
-        nc.vector.memset(tab_rows[:, :T // 2].bitcast(I32), 0)
         nc.gpsimd.memset(tab_rows[:, T // 2:].bitcast(I32), 0)
+        nc.vector.memset(tab_rows[:, :T // 2].bitcast(I32), 0)
         w2_scale_raw = held([P, PASSES, H], U8, "w2_scale_raw")
         nc.gpsimd.memset(w2_scale_raw[:].rearrange("p a c -> p (a c)").bitcast(I32), 0)
+        v_scale = [held([P, S], U8, f"v_scale{a}") for a in range(PASSES)]
+        for a in range(PASSES):
+            nc.vector.memset(v_scale[a][:].bitcast(I32), 0)
+        w3_scale = held([P, N], U8, "w3_scale")
+        nc.vector.memset(w3_scale[:].bitcast(I32), 0)
         warm = held([P, 3], F32, "warm")
         nc.vector.memset(warm[:, 0:1], 1.0)
         nc.scalar.activation(out=warm[:, 1:2], in_=warm[:, 0:1], func=ACT.Abs_reciprocal_sqrt)
 
-        w2_scale_rows = w2_scales.bitcast(I32).rearrange("a (Q r) c -> r Q a c", r=4)
-        second_rows = held([P, S], U8, "second_rows")
-        nc.vector.memset(second_rows[:].bitcast(I32), 0)
-        w3_scale = held([P, N], U8, "w3_scale")
-        nc.vector.memset(w3_scale[:].bitcast(I32), 0)
-
         w2_raw = held([P, PASSES, 2 * H], U8, "w2_raw")
         nc.sync.dma_start(out=w2_raw[:].bitcast(I32), in_=w2_words.bitcast(I32).rearrange("a p c -> p a c"))
-        nc.sync.dma_start(out=tab_rows[4:P:8, :].bitcast(I32), in_=tab_scales[1].bitcast(I32))
-        first_rows = tab_scales[0].bitcast(I32).rearrange("(Q r) c -> r Q c", r=4)
+        tab = [held([P, T], U32, f"tab{a}") for a in range(PASSES)]
+
+        def load_table(a, half):
+            part = slice(half * T // 2, (half + 1) * T // 2)
+            words = tab_words[a].rearrange("p t i -> p (t i)").bitcast(I32)
+            nc.sync.dma_start(out=tab[a][:, part].bitcast(I32), in_=words[:, part])
+
+        load_table(0, 0)
+        nc.sync.dma_start(
+            out=tab_rows[0:P:4, :].bitcast(I32), in_=tab_scales.bitcast(I32).rearrange("a q c -> (a q) c")
+        )
+        w2_scale_rows = w2_scales.bitcast(I32).rearrange("a (Q r) c -> r Q a c", r=4)
         for r in range(4):
-            nc.sync.dma_start(out=tab_rows[r:P:32, :].bitcast(I32), in_=first_rows[r])
+            nc.sync.dma_start(out=w2_scale_raw[r:P:32, :, :].bitcast(I32), in_=w2_scale_rows[r])
+
+        picked_rows = held([P, S], U8, "picked_rows")
+        nc.vector.tensor_copy(out=picked_rows[:], in_=tab_rows[:].indirect(picks[:]))
+
+        def place_scale_rows(a):
+            for r in range(4):
+                nc.sync.dma_start(
+                    out=v_scale[a][r:P:32, :].bitcast(I32),
+                    in_=picked_rows[64 * a + 4 * r:64 * a + 64:16, :].bitcast(I32),
+                )
+
+        load_table(0, 1)
+        load_table(1, 0)
+        place_scale_rows(0)
+        load_table(1, 1)
+        place_scale_rows(1)
+
         w1_raw = [held([P, PACK, H], F32, f"w1_raw{a}") for a in range(PASSES)]
         w1_rows = w1.rearrange("(a p j) c -> a p j c", a=PASSES, j=PACK)
-        tab = [held([P, T], U32, f"tab{a}") for a in range(PASSES)]
-        for a in range(PASSES):
-            nc.sync.dma_start(
-                out=tab[a][:].bitcast(I32),
-                in_=tab_words[a].rearrange("p t i -> p (t i)").bitcast(I32),
-            )
-            if a == 0:
-                for r in range(4):
-                    nc.sync.dma_start(out=w2_scale_raw[r:P:32, :, :].bitcast(I32), in_=w2_scale_rows[r])
-            nc.sync.dma_start(out=w1_raw[a][:], in_=w1_rows[a])
-        gain = [held([P, S], F32, f"gain{t}") for t in range(PACK)]
-        page = [held([P, T2], F32, f"page{t}") for t in range(PACK)]
-        gain_rows = wgs.rearrange("(q t) j -> t q j", t=PACK)
-        page_rows = page0.rearrange("(p t) c -> t p c", t=PACK)
-        for t in range(PACK):
-            early = BANK if t < 2 else S
+        gain = held([P, PACK * S], F32, "gain")
+        gain_rows = wgs.rearrange("(q t) j -> q (t j)", t=PACK)
+
+        def load_gain(t, h):
+            c0, c1 = t * S + h * BANK, t * S + (h + 1) * BANK
             for quad in (0, 2, 1, 3):
-                nc.sync.dma_start(out=gain[t][32 * quad:32 * quad + 32, :early], in_=gain_rows[t][:, :early])
-            if t == 0:
-                nc.sync.dma_start(places[:], offs2)
-            nc.sync.dma_start(out=page[t][:], in_=page_rows[t])
-            if early < S:
-                for quad in (0, 2, 1, 3):
-                    nc.sync.dma_start(out=gain[t][32 * quad:32 * quad + 32, early:], in_=gain_rows[t][:, early:])
+                nc.sync.dma_start(out=gain[32 * quad:32 * quad + 32, c0:c1], in_=gain_rows[:, c0:c1])
+
+        page = [held([P, T2], F32, f"page{t}") for t in range(PACK)]
+        page_rows = page0.rearrange("(p t) c -> t p c", t=PACK)
+        nc.sync.dma_start(out=w1_raw[0][:], in_=w1_rows[0])
+        nc.sync.dma_start(out=w1_raw[1][:], in_=w1_rows[1])
+        for t in range(0, PACK, 2):
+            for i in range(2):
+                load_gain(t + i, 0)
+                if t + i == 0:
+                    nc.sync.dma_start(places[:], offs2)
+                nc.sync.dma_start(out=page[t + i][:], in_=page_rows[t + i])
+            for i in range(2):
+                load_gain(t + i, 1)
         w3 = held([P, N], U32, "w3")
         nc.sync.dma_start(
             out=w3[:].bitcast(I32), in_=w3_words[0].rearrange("p c i -> p (c i)").bitcast(I32)
@@ -100,13 +122,6 @@ def tile_list_rehab_embedding_refresh_kernel(
         with nc.allow_non_contiguous_dma(reason="one bias value to a partition"):
             nc.sync.dma_start(out=bias[:], in_=b3.rearrange("(i p) -> p i", p=P))
 
-        picked_rows = held([P, S], U8, "picked_rows")
-        nc.vector.tensor_copy(out=picked_rows[:], in_=tab_rows[:].indirect(picks[:]))
-        for r in range(4):
-            nc.gpsimd.dma_start(
-                out=second_rows[r:P:32, :].bitcast(I32), in_=picked_rows[8 * r + 4:P:32, :].bitcast(I32)
-            )
-        v_scale = (picked_rows, second_rows)
         w2 = held([P, PASSES, 2 * H], U8, "w2")
         nc.vector.tensor_copy(
             out=w2[:].rearrange("p a (t m b) -> p a t m b", t=PACK, b=2),
@@ -126,34 +141,13 @@ def tile_list_rehab_embedding_refresh_kernel(
                     out=v[a][h][:], in_=tab[a][:].indirect(picks[:, h * cols:(h + 1) * cols])
                 )
 
-        w1_codes = held([P, PASSES, H], U32, "w1_codes")
-        w1_scale = held([P, PASSES, H], U8, "w1_scale")
-        for a in range(PASSES):
-            grouped = held([P, H * PACK], BF16, f"w1_grouped{a}")
-            dst = grouped[:].rearrange("p (t m j) -> p m j t", t=PACK, j=PACK)
-            src = w1_raw[a][:].rearrange("p j (m t) -> p m j t", t=PACK)
-            if a == 0:
-                nc.scalar.copy(out=dst, in_=src)
-                parts = ((0, H),)
-            else:
-                nc.vector.tensor_copy(out=dst, in_=src)
-                parts = ((0, P), (P, 2 * P), (2 * P, H))
-            for c0, c1 in parts:
-                nc.vector.quantize_mx(
-                    out=w1_codes[:, a, c0:c1].bitcast(FP8X4),
-                    scales=w1_scale[:, a, c0:c1],
-                    in_=grouped[:, PACK * c0:PACK * c1],
-                )
-
-        rounded = held([P, PACK, T2], BF16, "rounded")
-        out_rows = out_1.rearrange("(p t) c -> t p c", t=PACK)
-        def product(words, scales, dtype, width, t, h):
-            acc = psum.tile([P, BANK], F32, name="acc", bufs=3)
+        def product(words, scales, dtype, width, t, h, bank):
+            acc = psum.tile([P, BANK], F32, name="acc", tag=f"bank{bank}")
             for a in range(PASSES):
                 nc.tensor.matmul_mx(
                     out=acc[:],
-                    lhsT=words[:, a, width * t * P:width * (t + 1) * P].bitcast(dtype),
-                    lhsT_scale=scales[:, a, t * P:(t + 1) * P],
+                    lhsT=words[a][:, width * t * P:width * (t + 1) * P].bitcast(dtype),
+                    lhsT_scale=scales[a][:, t * P:(t + 1) * P],
                     rhs=v[a][h][:].bitcast(FP8X4),
                     rhs_scale=v_scale[a][:, h * BANK:(h + 1) * BANK],
                     start=(a == 0),
@@ -161,42 +155,78 @@ def tile_list_rehab_embedding_refresh_kernel(
                 )
             return acc
 
-        def damping(t, h):
-            acc_b = product(w2, w2_scale, FP4X4, 2, t, h)
-            size = w1_raw[0][:, (HALVES * t + h) % PACK, :]
-            nc.scalar.activation(out=size, in_=acc_b[:], func=ACT.Abs)
-            root = ring.tile([P, BANK], F32, name="root")
-            nc.scalar.activation(out=root[:], in_=size, func=ACT.Abs_reciprocal_sqrt, bias=1.0)
-            damp = ring.tile([P, BANK], F32, name="damp", bufs=4)
-            nc.scalar.activation(out=damp[:], in_=root[:], func=ACT.Square)
-            return damp
+        w2_passes = [w2[:, a, :] for a in range(PASSES)]
+        w2_scale_passes = [w2_scale[:, a, :] for a in range(PASSES)]
 
-        first_damps = [damping(0, h) for h in range(HALVES)]
-        for t in range(PACK):
-            fresh = held([P, S], F32, f"fresh{t}")
-            for h in range(HALVES):
-                picked = slice(h * BANK, (h + 1) * BANK)
-                damp = first_damps[h] if t == 0 else damping(t, h)
-                acc_a = product(w1_codes, w1_scale, FP8X4, 1, t, h)
-                partial = ring.tile([P, BANK], F32, name="partial")
-                if t == 0 and h == 0:
-                    nc.vector.tensor_tensor(out=partial[:], in0=damp[:], in1=gain[t][:, picked], op=MULT)
-                    nc.vector.tensor_tensor(out=fresh[:, picked], in0=acc_a[:], in1=partial[:], op=MULT)
-                else:
-                    raw = ring.tile([P, BANK], F32, name="raw", bufs=3)
-                    nc.scalar.copy(out=raw[:], in_=acc_a[:])
-                    nc.gpsimd.tensor_tensor(out=partial[:], in0=raw[:], in1=damp[:], op=MULT)
-                    nc.gpsimd.tensor_tensor(out=fresh[:, picked], in0=partial[:], in1=gain[t][:, picked], op=MULT)
-                if t < 2:
-                    nc.vector.tensor_copy(
-                        out=page[t][:].indirect(places[:, h * cols:(h + 1) * cols]), in_=fresh[:, picked]
-                    )
-            if t >= 2:
-                nc.vector.tensor_copy(out=page[t][:].indirect(places[:]), in_=fresh[:])
-            nc.sync.dma_start(out=out_rows[t], in_=page[t][:])
+        units = [(t + i, h) for t in range(0, PACK, 2) for h in range(HALVES) for i in range(2)]
+        size, damp = {}, {}
+
+        def size_of_b(u):
+            acc_b = product(w2_passes, w2_scale_passes, FP4X4, 2, *units[u], u % 5)
+            size[u] = held([P, BANK], F32, "size")
+            nc.scalar.activation(out=size[u][:], in_=acc_b[:], func=ACT.Abs)
+
+        def inverse_root(u):
+            if u == 1:
+                damp[u] = keep.tile([P, BANK], F32, name="damp1", tag="w1_raw1", align_bytes=64)
+            else:
+                damp[u] = ring.tile([P, BANK], F32, name="damp", bufs=2)
+            nc.scalar.activation(out=damp[u][:], in_=size[u][:], func=ACT.Abs_reciprocal_sqrt, bias=1.0)
+
+        def squared(u):
+            nc.scalar.activation(out=damp[u][:], in_=damp[u][:], func=ACT.Square)
+
+        size_of_b(0)
+        inverse_root(0)
+        size_of_b(1)
+        squared(0)
+
+        w1_codes = [held([P, H], U32, f"w1_codes{a}") for a in range(PASSES)]
+        w1_scale = [held([P, H], U8, f"w1_scale{a}") for a in range(PASSES)]
+        first_factor = held([P, BANK], F32, "first_factor")
+        for a in range(PASSES):
+            grouped = held([P, H * PACK], BF16, f"w1_grouped{a}")
+            dst = grouped[:].rearrange("p (t m j) -> p m j t", t=PACK, j=PACK)
+            src = w1_raw[a][:].rearrange("p j (m t) -> p m j t", t=PACK)
+            if a == 0:
+                nc.vector.tensor_copy(out=dst, in_=src)
+            else:
+                nc.vector.tensor_copy(out=dst[:, :88], in_=src[:, :88])
+                nc.scalar.copy(out=dst[:, 88:], in_=src[:, 88:])
+                inverse_root(1)
+                nc.vector.tensor_tensor(out=first_factor[:], in0=damp[0][:], in1=gain[:, :BANK], op=MULT)
+            for c0, c1 in ((0, H),) if a == 0 else ((0, P), (P, 2 * P), (2 * P, H)):
+                nc.vector.quantize_mx(
+                    out=w1_codes[a][:, c0:c1].bitcast(FP8X4),
+                    scales=w1_scale[a][:, c0:c1],
+                    in_=grouped[:, PACK * c0:PACK * c1],
+                )
+
+        out_rows = out_1.rearrange("(p t) c -> t p c", t=PACK)
+        for u, (t, h) in enumerate(units):
+            fresh = held([P, BANK], F32, f"fresh{u}")[:]
+            acc_a = product(w1_codes, w1_scale, FP8X4, 1, t, h, (u + 3) % 5)
+            if u == 0:
+                nc.vector.tensor_tensor(out=fresh, in0=acc_a[:], in1=first_factor[:], op=MULT)
+            else:
+                if u + 1 < len(units):
+                    size_of_b(u + 1)
+                squared(u)
+                if u + 1 < len(units):
+                    inverse_root(u + 1)
+                raw = ring.tile([P, BANK], F32, name="raw", bufs=4)
+                nc.scalar.copy(out=raw[:], in_=acc_a[:])
+                partial = ring.tile([P, BANK], F32, name="partial", bufs=1)
+                nc.gpsimd.tensor_tensor(out=partial[:], in0=raw[:], in1=damp[u][:], op=MULT)
+                c0 = t * S + h * BANK
+                nc.gpsimd.tensor_tensor(out=fresh, in0=partial[:], in1=gain[:, c0:c0 + BANK], op=MULT)
+            nc.vector.tensor_copy(out=page[t][:].indirect(places[:, h * cols:(h + 1) * cols]), in_=fresh)
+            if h == HALVES - 1:
+                nc.sync.dma_start(out=out_rows[t], in_=page[t][:])
+        nc.scalar.activation(out=warm[:, 2:3], in_=damp[len(units) - 1][:, 0:1], func=ACT.Tanh)
+        rounded = keep.tile([P, PACK, T2], BF16, name="rounded", tag="size", align_bytes=64)
         for t in range(PACK - 1):
             nc.scalar.copy(out=rounded[:, t, :], in_=page[t][:])
-        nc.scalar.activation(out=warm[:, 2:3], in_=damp[:, 0:1], func=ACT.Tanh)
 
         codes = held([P, T2], U32, "codes")
         scale = held([P, T2], U8, "scale")
@@ -224,6 +254,7 @@ def tile_list_rehab_embedding_refresh_kernel(
                     in_=woven[:, lo:hi, :].rearrange("p c t -> p (c t)"),
                 )
 
+        next_bank = [0]
         for s0, s1, space in ((0, BANK, "features"), (BANK, 2 * BANK, "tab1"), (2 * BANK, T2, "tab0")):
             for c0 in range(s0, s1, BANK):
                 quantise(c0)
@@ -239,7 +270,8 @@ def tile_list_rehab_embedding_refresh_kernel(
                 rows = slice(i * P, (i + 1) * P)
                 for c0 in range(s0, s1, BANK):
                     chunk = slice(c0, c0 + BANK)
-                    acc_c = psum.tile([P, BANK], F32, name="acc_c", bufs=5)
+                    acc_c = psum.tile([P, BANK], F32, name="acc_c", tag=f"bank{next_bank[0] % 8}")
+                    next_bank[0] += 1
                     nc.tensor.matmul_mx(
                         out=acc_c[:],
                         lhsT=w3[:, rows].bitcast(FP8X4),

@@ -56,19 +56,20 @@ def tile_list_rehab_embedding_refresh_kernel(
         nc.vector.memset(warm[:, 0:1], 1.0)
         nc.scalar.activation(out=warm[:, 1:2], in_=warm[:, 0:1], func=ACT.Abs_reciprocal_sqrt)
 
-        w2_raw = held([P, PASSES, 2 * H], U8, "w2_raw")
-        nc.sync.dma_start(out=w2_raw[:].bitcast(I32), in_=w2_words.bitcast(I32).rearrange("a p c -> p a c"))
         tab = [held([P, T], U32, f"tab{a}") for a in range(PASSES)]
 
-        def load_table(a, half):
-            part = slice(half * T // 2, (half + 1) * T // 2)
+        def load_table(a, piece):
+            cut = (T // 4, T // 2)[a]
+            part = (slice(0, cut), slice(cut, T))[piece]
             words = tab_words[a].rearrange("p t i -> p (t i)").bitcast(I32)
             nc.sync.dma_start(out=tab[a][:, part].bitcast(I32), in_=words[:, part])
 
         load_table(0, 0)
         nc.sync.dma_start(
-            out=tab_rows[0:P:4, :].bitcast(I32), in_=tab_scales.bitcast(I32).rearrange("a q c -> (a q) c")
+            out=tab_rows[32:96:2, :].bitcast(I32), in_=tab_scales.bitcast(I32).rearrange("a q c -> (a q) c")
         )
+        w2_raw = held([P, PASSES, 2 * H], U8, "w2_raw")
+        nc.sync.dma_start(out=w2_raw[:].bitcast(I32), in_=w2_words.bitcast(I32).rearrange("a p c -> p a c"))
         w2_scale_rows = w2_scales.bitcast(I32).rearrange("a (Q r) c -> r Q a c", r=4)
         for r in range(4):
             nc.sync.dma_start(out=w2_scale_raw[r:P:32, :, :].bitcast(I32), in_=w2_scale_rows[r])
@@ -80,7 +81,7 @@ def tile_list_rehab_embedding_refresh_kernel(
             for r in range(4):
                 nc.sync.dma_start(
                     out=v_scale[a][r:P:32, :].bitcast(I32),
-                    in_=picked_rows[64 * a + 4 * r:64 * a + 64:16, :].bitcast(I32),
+                    in_=picked_rows[32 * a + 32 + 2 * r:32 * a + 64:8, :].bitcast(I32),
                 )
 
         load_table(0, 1)
@@ -254,24 +255,30 @@ def tile_list_rehab_embedding_refresh_kernel(
                     in_=woven[:, lo:hi, :].rearrange("p c t -> p (c t)"),
                 )
 
-        next_bank = [0]
-        for s0, s1, space in ((0, BANK, "features"), (BANK, 2 * BANK, "tab1"), (2 * BANK, T2, "tab0")):
+        banks = list(range(8)) * 3
+        out_tiles = out_0.rearrange("(i p) c -> p i c", p=P)
+        spans = (
+            (0, BANK, "features", (1, 2, 4, 6)),
+            (BANK, 2 * BANK, "tab1", (3, 6)),
+            (2 * BANK, T2, "tab0", (2, 4, 5, 6)),
+        )
+        for s0, s1, space, ends in spans:
             for c0 in range(s0, s1, BANK):
                 quantise(c0)
             nc.sync.dma_start(out=code_rows[:, s0:s1], in_=codes[:, s0:s1].bitcast(I32))
             if s1 == T2:
                 for quad in range(QUADS):
-                    nc.sync.dma_start(
+                    nc.gpsimd.dma_start(
                         out=scale_rows[4 * quad:4 * quad + 4, :],
                         in_=scale[32 * quad:32 * quad + 4, :].bitcast(I32),
                     )
             features = keep.tile([P, N_TILES, s1 - s0], F32, name=f"features{s0}", tag=space, align_bytes=64)
+            stored = 0
             for i in range(N_TILES):
                 rows = slice(i * P, (i + 1) * P)
                 for c0 in range(s0, s1, BANK):
                     chunk = slice(c0, c0 + BANK)
-                    acc_c = psum.tile([P, BANK], F32, name="acc_c", tag=f"bank{next_bank[0] % 8}")
-                    next_bank[0] += 1
+                    acc_c = psum.tile([P, BANK], F32, name="acc_c", tag=f"bank{banks.pop()}")
                     nc.tensor.matmul_mx(
                         out=acc_c[:],
                         lhsT=w3[:, rows].bitcast(FP8X4),
@@ -284,4 +291,6 @@ def tile_list_rehab_embedding_refresh_kernel(
                     nc.scalar.activation(
                         out=features[:, i, c0 - s0:c0 - s0 + BANK], in_=acc_c[:], func=ACT.Tanh, bias=bias[:, i:i + 1]
                     )
-                nc.sync.dma_start(out=out_0[rows, s0:s1], in_=features[:, i, :])
+                if i + 1 in ends:
+                    nc.sync.dma_start(out=out_tiles[:, stored:i + 1, s0:s1], in_=features[:, stored:i + 1, :])
+                    stored = i + 1

@@ -40,7 +40,6 @@ def tile_list_rehab_embedding_refresh_kernel(
 
         picks = keep.tile([P, S // 16], U16, name="picks")
         places = keep.tile([P, S // 16], U16, name="places")
-        nc.sync.dma_start(picks[:], offs)
 
         tab_rows = held([P, T], U8, "tab_rows")
         nc.gpsimd.memset(tab_rows[:, T // 2:].bitcast(I32), 0)
@@ -64,6 +63,7 @@ def tile_list_rehab_embedding_refresh_kernel(
             words = tab_words[a].rearrange("p t i -> p (t i)").bitcast(I32)
             nc.sync.dma_start(out=tab[a][:, part].bitcast(I32), in_=words[:, part])
 
+        nc.sync.dma_start(picks[:], offs)
         load_table(0, 0)
         nc.sync.dma_start(
             out=tab_rows[32:96:2, :].bitcast(I32), in_=tab_scales.bitcast(I32).rearrange("a q c -> (a q) c")
@@ -95,8 +95,7 @@ def tile_list_rehab_embedding_refresh_kernel(
         gain = held([P, PACK * S], F32, "gain")
         gain_rows = wgs.rearrange("(q t) j -> q (t j)", t=PACK)
 
-        def load_gain(t, h):
-            c0, c1 = t * S + h * BANK, t * S + (h + 1) * BANK
+        def load_gain(c0, c1):
             for quad in (0, 2, 1, 3):
                 nc.sync.dma_start(out=gain[32 * quad:32 * quad + 32, c0:c1], in_=gain_rows[:, c0:c1])
 
@@ -106,12 +105,12 @@ def tile_list_rehab_embedding_refresh_kernel(
         nc.sync.dma_start(out=w1_raw[1][:], in_=w1_rows[1])
         for t in range(0, PACK, 2):
             for i in range(2):
-                load_gain(t + i, 0)
+                load_gain((t + i) * S, (t + i) * S + BANK)
                 if t + i == 0:
                     nc.sync.dma_start(places[:], offs2)
                 nc.sync.dma_start(out=page[t + i][:], in_=page_rows[t + i])
             for i in range(2):
-                load_gain(t + i, 1)
+                load_gain((t + i) * S + BANK, (t + i + 1) * S)
         w3 = held([P, N], U32, "w3")
         nc.sync.dma_start(
             out=w3[:].bitcast(I32), in_=w3_words[0].rearrange("p c i -> p (c i)").bitcast(I32)
@@ -164,14 +163,11 @@ def tile_list_rehab_embedding_refresh_kernel(
 
         def size_of_b(u):
             acc_b = product(w2_passes, w2_scale_passes, FP4X4, 2, *units[u], u % 5)
-            size[u] = held([P, BANK], F32, "size")
+            size[u] = held([P, BANK], F32, "w1_raw1" if u else "first_size")
             nc.scalar.activation(out=size[u][:], in_=acc_b[:], func=ACT.Abs)
 
         def inverse_root(u):
-            if u == 1:
-                damp[u] = keep.tile([P, BANK], F32, name="damp1", tag="w1_raw1", align_bytes=64)
-            else:
-                damp[u] = ring.tile([P, BANK], F32, name="damp", bufs=2)
+            damp[u] = ring.tile([P, BANK], F32, name="damp", bufs=3)
             nc.scalar.activation(out=damp[u][:], in_=size[u][:], func=ACT.Abs_reciprocal_sqrt, bias=1.0)
 
         def squared(u):
@@ -179,7 +175,6 @@ def tile_list_rehab_embedding_refresh_kernel(
 
         size_of_b(0)
         inverse_root(0)
-        size_of_b(1)
         squared(0)
 
         w1_codes = [held([P, H], U32, f"w1_codes{a}") for a in range(PASSES)]
@@ -194,6 +189,7 @@ def tile_list_rehab_embedding_refresh_kernel(
             else:
                 nc.vector.tensor_copy(out=dst[:, :88], in_=src[:, :88])
                 nc.scalar.copy(out=dst[:, 88:], in_=src[:, 88:])
+                size_of_b(1)
                 inverse_root(1)
                 nc.vector.tensor_tensor(out=first_factor[:], in0=damp[0][:], in1=gain[:, :BANK], op=MULT)
             for c0, c1 in ((0, H),) if a == 0 else ((0, P), (P, 2 * P), (2 * P, H)):
@@ -210,22 +206,27 @@ def tile_list_rehab_embedding_refresh_kernel(
             if u == 0:
                 nc.vector.tensor_tensor(out=fresh, in0=acc_a[:], in1=first_factor[:], op=MULT)
             else:
-                if u + 1 < len(units):
-                    size_of_b(u + 1)
-                squared(u)
-                if u + 1 < len(units):
-                    inverse_root(u + 1)
                 raw = ring.tile([P, BANK], F32, name="raw", bufs=4)
-                nc.scalar.copy(out=raw[:], in_=acc_a[:])
+                if u == 1:
+                    squared(u)
+                    nc.scalar.copy(out=raw[:], in_=acc_a[:])
+                    size_of_b(u + 1)
+                    inverse_root(u + 1)
+                else:
+                    if u + 1 < len(units):
+                        size_of_b(u + 1)
+                    squared(u)
+                    if u + 1 < len(units):
+                        inverse_root(u + 1)
+                    nc.scalar.copy(out=raw[:], in_=acc_a[:])
                 partial = ring.tile([P, BANK], F32, name="partial", bufs=1)
                 nc.gpsimd.tensor_tensor(out=partial[:], in0=raw[:], in1=damp[u][:], op=MULT)
-                c0 = t * S + h * BANK
-                nc.gpsimd.tensor_tensor(out=fresh, in0=partial[:], in1=gain[:, c0:c0 + BANK], op=MULT)
+                nc.gpsimd.tensor_tensor(out=fresh, in0=partial[:], in1=gain[:, t * S + h * BANK:t * S + (h + 1) * BANK], op=MULT)
             nc.vector.tensor_copy(out=page[t][:].indirect(places[:, h * cols:(h + 1) * cols]), in_=fresh)
             if h == HALVES - 1:
                 nc.sync.dma_start(out=out_rows[t], in_=page[t][:])
         nc.scalar.activation(out=warm[:, 2:3], in_=damp[len(units) - 1][:, 0:1], func=ACT.Tanh)
-        rounded = keep.tile([P, PACK, T2], BF16, name="rounded", tag="size", align_bytes=64)
+        rounded = keep.tile([P, PACK, T2], BF16, name="rounded", tag="w1_raw1", align_bytes=64)
         for t in range(PACK - 1):
             nc.scalar.copy(out=rounded[:, t, :], in_=page[t][:])
 
@@ -255,12 +256,27 @@ def tile_list_rehab_embedding_refresh_kernel(
                     in_=woven[:, lo:hi, :].rearrange("p c t -> p (c t)"),
                 )
 
-        banks = list(range(8)) * 3
+        banks = list(range(8)) * 4
         out_tiles = out_0.rearrange("(i p) c -> p i c", p=P)
+
+        def features(i, c0, c1, out):
+            rows = slice(i * P, (i + 1) * P)
+            acc_c = psum.tile([P, BANK], F32, name="acc_c", tag=f"bank{banks.pop()}")
+            nc.tensor.matmul_mx(
+                out=acc_c[:, :c1 - c0],
+                lhsT=w3[:, rows].bitcast(FP8X4),
+                lhsT_scale=w3_scale[:, rows],
+                rhs=codes[:, c0:c1].bitcast(FP8X4),
+                rhs_scale=scale[:, c0:c1],
+                start=True,
+                stop=True,
+            )
+            nc.scalar.activation(out=out, in_=acc_c[:, :c1 - c0], func=ACT.Tanh, bias=bias[:, i:i + 1])
+
         spans = (
-            (0, BANK, "features", (1, 2, 4, 6)),
-            (BANK, 2 * BANK, "tab1", (3, 6)),
-            (2 * BANK, T2, "tab0", (2, 4, 5, 6)),
+            (0, BANK, "features", (1, 2, 3, 4, 5, 6)),
+            (BANK, 2 * BANK, "tab1", (2, 4, 6)),
+            (2 * BANK, T2, "tab0", (1, 2, 3, 4, 5, 6)),
         )
         for s0, s1, space, ends in spans:
             for c0 in range(s0, s1, BANK):
@@ -272,25 +288,19 @@ def tile_list_rehab_embedding_refresh_kernel(
                         out=scale_rows[4 * quad:4 * quad + 4, :],
                         in_=scale[32 * quad:32 * quad + 4, :].bitcast(I32),
                     )
-            features = keep.tile([P, N_TILES, s1 - s0], F32, name=f"features{s0}", tag=space, align_bytes=64)
+            result = keep.tile([P, N_TILES, s1 - s0], F32, name=f"features{s0}", tag=space, align_bytes=64)
+            early = 3 if s0 == 0 else 0
+            for i in range(early):
+                features(i, 0, BANK // 2, result[:, i, :BANK // 2])
             stored = 0
             for i in range(N_TILES):
-                rows = slice(i * P, (i + 1) * P)
                 for c0 in range(s0, s1, BANK):
-                    chunk = slice(c0, c0 + BANK)
-                    acc_c = psum.tile([P, BANK], F32, name="acc_c", tag=f"bank{banks.pop()}")
-                    nc.tensor.matmul_mx(
-                        out=acc_c[:],
-                        lhsT=w3[:, rows].bitcast(FP8X4),
-                        lhsT_scale=w3_scale[:, rows],
-                        rhs=codes[:, chunk].bitcast(FP8X4),
-                        rhs_scale=scale[:, chunk],
-                        start=True,
-                        stop=True,
-                    )
-                    nc.scalar.activation(
-                        out=features[:, i, c0 - s0:c0 - s0 + BANK], in_=acc_c[:], func=ACT.Tanh, bias=bias[:, i:i + 1]
-                    )
-                if i + 1 in ends:
-                    nc.sync.dma_start(out=out_tiles[:, stored:i + 1, s0:s1], in_=features[:, stored:i + 1, :])
+                    lo = BANK // 2 if i < early else c0
+                    features(i, lo, c0 + BANK, result[:, i, lo - s0:c0 - s0 + BANK])
+                    if True and s1 == T2 and i == N_TILES - 1:
+                        nc.sync.dma_start(
+                            out=out_tiles[:, i, c0:c0 + BANK], in_=result[:, i, c0 - s0:c0 - s0 + BANK]
+                        )
+                if i + 1 in ends and not (True and s1 == T2 and i == N_TILES - 1):
+                    nc.sync.dma_start(out=out_tiles[:, stored:i + 1, s0:s1], in_=result[:, stored:i + 1, :])
                     stored = i + 1

@@ -274,9 +274,9 @@ def tile_list_rehab_embedding_refresh_kernel(
             nc.scalar.activation(out=out, in_=acc_c[:, :c1 - c0], func=ACT.Tanh, bias=bias[:, i:i + 1])
 
         spans = (
-            (0, BANK, "features", (1, 2, 3, 4, 5, 6)),
-            (BANK, 2 * BANK, "tab1", (2, 4, 6)),
-            (2 * BANK, T2, "tab0", (1, 2, 3, 4, 5, 6)),
+            (0, BANK, "features", (1, 2, 4, 6)),
+            (BANK, 2 * BANK, "tab1", (3, 6)),
+            (2 * BANK, T2, "tab0", (2, 4, 6)),
         )
         for s0, s1, space, ends in spans:
             for c0 in range(s0, s1, BANK):
@@ -297,10 +297,6 @@ def tile_list_rehab_embedding_refresh_kernel(
                 for c0 in range(s0, s1, BANK):
                     lo = BANK // 2 if i < early else c0
                     features(i, lo, c0 + BANK, result[:, i, lo - s0:c0 - s0 + BANK])
-                    if True and s1 == T2 and i == N_TILES - 1:
-                        nc.sync.dma_start(
-                            out=out_tiles[:, i, c0:c0 + BANK], in_=result[:, i, c0 - s0:c0 - s0 + BANK]
-                        )
-                if i + 1 in ends and not (True and s1 == T2 and i == N_TILES - 1):
+                if i + 1 in ends:
                     nc.sync.dma_start(out=out_tiles[:, stored:i + 1, s0:s1], in_=result[:, stored:i + 1, :])
                     stored = i + 1

@@ -1,6 +1,7 @@
 from contextlib import ExitStack
 
 import concourse.mybir as mybir
+from concourse.masks import make_identity
 
 K, T, S, T2, H, N = 1024, 4096, 1024, 2048, 512, 768
 FLOPS = 2 * 2 * K * H * S + 2 * H * N * T2
@@ -33,6 +34,7 @@ def tile_list_rehab_embedding_refresh_kernel(
     with ExitStack() as ctx:
         keep = ctx.enter_context(tc.tile_pool(name="keep", bufs=1))
         ring = ctx.enter_context(tc.tile_pool(name="ring", bufs=2))
+        reuse = ctx.enter_context(tc.tile_pool(name="reuse", bufs=1))
         psum = ctx.enter_context(tc.psum_pool(name="psum", bufs=1))
 
         def held(shape, dtype, name):
@@ -57,19 +59,18 @@ def tile_list_rehab_embedding_refresh_kernel(
 
         tab = [held([P, T], U32, f"tab{a}") for a in range(PASSES)]
 
-        def load_table(a, piece):
-            cut = (T // 4, T // 2)[a]
-            part = (slice(0, cut), slice(cut, T))[piece]
+        def load_table(a, part):
             words = tab_words[a].rearrange("p t i -> p (t i)").bitcast(I32)
             nc.sync.dma_start(out=tab[a][:, part].bitcast(I32), in_=words[:, part])
 
         nc.sync.dma_start(picks[:], offs)
-        load_table(0, 0)
+        gain_head = held([P, BANK], F32, "gain_head")
+        nc.sync.dma_start(out=gain_head[:], in_=wgs[:, :BANK])
+        w2_raw = held([P, PASSES, 2 * H], U8, "w2_raw")
+        nc.sync.dma_start(out=w2_raw[:].bitcast(I32), in_=w2_words.bitcast(I32).rearrange("a p c -> p a c"))
         nc.sync.dma_start(
             out=tab_rows[32:96:2, :].bitcast(I32), in_=tab_scales.bitcast(I32).rearrange("a q c -> (a q) c")
         )
-        w2_raw = held([P, PASSES, 2 * H], U8, "w2_raw")
-        nc.sync.dma_start(out=w2_raw[:].bitcast(I32), in_=w2_words.bitcast(I32).rearrange("a p c -> p a c"))
         w2_scale_rows = w2_scales.bitcast(I32).rearrange("a (Q r) c -> r Q a c", r=4)
         for r in range(4):
             nc.sync.dma_start(out=w2_scale_raw[r:P:32, :, :].bitcast(I32), in_=w2_scale_rows[r])
@@ -84,33 +85,34 @@ def tile_list_rehab_embedding_refresh_kernel(
                     in_=picked_rows[32 * a + 32 + 2 * r:32 * a + 64:8, :].bitcast(I32),
                 )
 
-        load_table(0, 1)
-        load_table(1, 0)
+        load_table(0, slice(0, T))
+        load_table(1, slice(0, T // 2))
         place_scale_rows(0)
-        load_table(1, 1)
+        load_table(1, slice(T // 2, T))
         place_scale_rows(1)
 
-        w1_raw = [held([P, PACK, H], F32, f"w1_raw{a}") for a in range(PASSES)]
+        w1_raw = [held([P, PACK, H], F32, "w1_raw0"), reuse.tile([P, PACK, H], F32, name="w1_raw1", offset=0)]
         w1_rows = w1.rearrange("(a p j) c -> a p j c", a=PASSES, j=PACK)
-        gain = held([P, PACK * S], F32, "gain")
+        gain = [held([P, PACK * BANK], F32, f"gain{h}") for h in range(HALVES)]
         gain_rows = wgs.rearrange("(q t) j -> q (t j)", t=PACK)
 
-        def load_gain(c0, c1):
+        def load_gain(t):
             for quad in (0, 2, 1, 3):
-                nc.sync.dma_start(out=gain[32 * quad:32 * quad + 32, c0:c1], in_=gain_rows[:, c0:c1])
+                nc.sync.dma_start(
+                    out=gain[1][32 * quad:32 * quad + 32, t * BANK:(t + 1) * BANK],
+                    in_=gain_rows[:, t * S + BANK:(t + 1) * S],
+                )
 
         page = [held([P, T2], F32, f"page{t}") for t in range(PACK)]
         page_rows = page0.rearrange("(p t) c -> t p c", t=PACK)
         nc.sync.dma_start(out=w1_raw[0][:], in_=w1_rows[0])
         nc.sync.dma_start(out=w1_raw[1][:], in_=w1_rows[1])
+        nc.sync.dma_start(places[:], offs2)
         for t in range(0, PACK, 2):
             for i in range(2):
-                load_gain((t + i) * S, (t + i) * S + BANK)
-                if t + i == 0:
-                    nc.sync.dma_start(places[:], offs2)
                 nc.sync.dma_start(out=page[t + i][:], in_=page_rows[t + i])
             for i in range(2):
-                load_gain((t + i) * S + BANK, (t + i + 1) * S)
+                load_gain(t + i)
         w3 = held([P, N], U32, "w3")
         nc.sync.dma_start(
             out=w3[:].bitcast(I32), in_=w3_words[0].rearrange("p c i -> p (c i)").bitcast(I32)
@@ -132,6 +134,25 @@ def tile_list_rehab_embedding_refresh_kernel(
             out=w2_scale[:].rearrange("p a (t m) -> p a t m", t=PACK),
             in_=w2_scale_raw[:].rearrange("p a (m t) -> p a t m", t=PACK),
         )
+
+        identity = held([P, P], F32, "identity")
+        make_identity(nc, identity[:])
+        blocks = [slice(j0, j0 + P) for j0 in range(0, BANK, P)]
+        flipped = psum.tile([P, BANK], F32, name="flipped", tag="bank7")
+        for block in blocks:
+            nc.tensor.transpose(flipped[:, block], gain_head[:, block], identity[:])
+        dealt = held([P, len(blocks), PACK, P], F32, "dealt")
+        for j, block in enumerate(blocks):
+            rows = flipped[:, block].rearrange("p (q t) -> p t q", t=PACK)
+            nc.scalar.copy(
+                out=dealt[:, j].rearrange("p t (c q) -> p t c q", c=QUADS),
+                in_=rows.unsqueeze(2).to_broadcast([P, PACK, QUADS, P // QUADS]),
+            )
+        for t in range(PACK):
+            back = psum.tile([P, BANK], F32, name="back", tag=f"bank{5 + t % 2}")
+            for j, block in enumerate(blocks):
+                nc.tensor.transpose(back[:, block], dealt[:, j, t, :], identity[:])
+            nc.scalar.copy(out=gain[0][:, t * BANK:(t + 1) * BANK], in_=back[:])
 
         cols = BANK // 16
         v = [[held([P, BANK], U32, f"v{a}_{h}") for h in range(HALVES)] for a in range(PASSES)]
@@ -163,7 +184,10 @@ def tile_list_rehab_embedding_refresh_kernel(
 
         def size_of_b(u):
             acc_b = product(w2_passes, w2_scale_passes, FP4X4, 2, *units[u], u % 5)
-            size[u] = held([P, BANK], F32, "w1_raw1" if u else "first_size")
+            if u:
+                size[u] = reuse.tile([P, BANK], F32, name=f"size{u}", offset=0)
+            else:
+                size[u] = held([P, BANK], F32, "first_size")
             nc.scalar.activation(out=size[u][:], in_=acc_b[:], func=ACT.Abs)
 
         def inverse_root(u):
@@ -179,7 +203,7 @@ def tile_list_rehab_embedding_refresh_kernel(
 
         w1_codes = [held([P, H], U32, f"w1_codes{a}") for a in range(PASSES)]
         w1_scale = [held([P, H], U8, f"w1_scale{a}") for a in range(PASSES)]
-        first_factor = held([P, BANK], F32, "first_factor")
+        first_factor = reuse.tile([P, BANK], F32, name="first_factor", offset=4 * BANK)
         for a in range(PASSES):
             grouped = held([P, H * PACK], BF16, f"w1_grouped{a}")
             dst = grouped[:].rearrange("p (t m j) -> p m j t", t=PACK, j=PACK)
@@ -191,13 +215,14 @@ def tile_list_rehab_embedding_refresh_kernel(
                 nc.scalar.copy(out=dst[:, 88:], in_=src[:, 88:])
                 size_of_b(1)
                 inverse_root(1)
-                nc.vector.tensor_tensor(out=first_factor[:], in0=damp[0][:], in1=gain[:, :BANK], op=MULT)
             for c0, c1 in ((0, H),) if a == 0 else ((0, P), (P, 2 * P), (2 * P, H)):
                 nc.vector.quantize_mx(
                     out=w1_codes[a][:, c0:c1].bitcast(FP8X4),
                     scales=w1_scale[a][:, c0:c1],
                     in_=grouped[:, PACK * c0:PACK * c1],
                 )
+                if a == 1 and c0 == P:
+                    nc.vector.tensor_tensor(out=first_factor[:], in0=damp[0][:], in1=gain[0][:, :BANK], op=MULT)
 
         out_rows = out_1.rearrange("(p t) c -> t p c", t=PACK)
         for u, (t, h) in enumerate(units):
@@ -220,13 +245,14 @@ def tile_list_rehab_embedding_refresh_kernel(
                         inverse_root(u + 1)
                     nc.scalar.copy(out=raw[:], in_=acc_a[:])
                 partial = ring.tile([P, BANK], F32, name="partial", bufs=1)
-                nc.gpsimd.tensor_tensor(out=partial[:], in0=raw[:], in1=damp[u][:], op=MULT)
-                nc.gpsimd.tensor_tensor(out=fresh, in0=partial[:], in1=gain[:, t * S + h * BANK:t * S + (h + 1) * BANK], op=MULT)
+                factors = (gain[h][:, t * BANK:(t + 1) * BANK], raw[:])
+                nc.gpsimd.tensor_tensor(out=partial[:], in0=damp[u][:], in1=factors[h], op=MULT)
+                nc.gpsimd.tensor_tensor(out=fresh, in0=partial[:], in1=factors[1 - h], op=MULT)
             nc.vector.tensor_copy(out=page[t][:].indirect(places[:, h * cols:(h + 1) * cols]), in_=fresh)
             if h == HALVES - 1:
                 nc.sync.dma_start(out=out_rows[t], in_=page[t][:])
         nc.scalar.activation(out=warm[:, 2:3], in_=damp[len(units) - 1][:, 0:1], func=ACT.Tanh)
-        rounded = keep.tile([P, PACK, T2], BF16, name="rounded", tag="w1_raw1", align_bytes=64)
+        rounded = reuse.tile([P, PACK, T2], BF16, name="rounded", offset=0)
         for t in range(PACK - 1):
             nc.scalar.copy(out=rounded[:, t, :], in_=page[t][:])
 

@@ -184,14 +184,14 @@ def tile_list_rehab_embedding_refresh_kernel(
 
         def size_of_b(u):
             acc_b = product(w2_passes, w2_scale_passes, FP4X4, 2, *units[u], u % 5)
-            if u:
-                size[u] = reuse.tile([P, BANK], F32, name=f"size{u}", offset=0)
-            else:
-                size[u] = held([P, BANK], F32, "first_size")
+            size[u] = held([P, BANK], F32, "size")
             nc.scalar.activation(out=size[u][:], in_=acc_b[:], func=ACT.Abs)
 
         def inverse_root(u):
-            damp[u] = ring.tile([P, BANK], F32, name="damp", bufs=3)
+            if u == 1:
+                damp[u] = reuse.tile([P, BANK], F32, name="second_damp", offset=0)
+            else:
+                damp[u] = ring.tile([P, BANK], F32, name="damp", bufs=2)
             nc.scalar.activation(out=damp[u][:], in_=size[u][:], func=ACT.Abs_reciprocal_sqrt, bias=1.0)
 
         def squared(u):
@@ -199,6 +199,7 @@ def tile_list_rehab_embedding_refresh_kernel(
 
         size_of_b(0)
         inverse_root(0)
+        size_of_b(1)
         squared(0)
 
         w1_codes = [held([P, H], U32, f"w1_codes{a}") for a in range(PASSES)]
@@ -211,9 +212,8 @@ def tile_list_rehab_embedding_refresh_kernel(
             if a == 0:
                 nc.vector.tensor_copy(out=dst, in_=src)
             else:
-                nc.vector.tensor_copy(out=dst[:, :88], in_=src[:, :88])
-                nc.scalar.copy(out=dst[:, 88:], in_=src[:, 88:])
-                size_of_b(1)
+                nc.vector.tensor_copy(out=dst[:, :96], in_=src[:, :96])
+                nc.scalar.copy(out=dst[:, 96:], in_=src[:, 96:])
                 inverse_root(1)
             for c0, c1 in ((0, H),) if a == 0 else ((0, P), (P, 2 * P), (2 * P, H)):
                 nc.vector.quantize_mx(
@@ -246,13 +246,13 @@ def tile_list_rehab_embedding_refresh_kernel(
                     nc.scalar.copy(out=raw[:], in_=acc_a[:])
                 partial = ring.tile([P, BANK], F32, name="partial", bufs=1)
                 factors = (gain[h][:, t * BANK:(t + 1) * BANK], raw[:])
-                nc.gpsimd.tensor_tensor(out=partial[:], in0=damp[u][:], in1=factors[h], op=MULT)
-                nc.gpsimd.tensor_tensor(out=fresh, in0=partial[:], in1=factors[1 - h], op=MULT)
+                nc.gpsimd.tensor_tensor(out=partial[:], in0=damp[u][:], in1=factors[u != 1], op=MULT)
+                nc.gpsimd.tensor_tensor(out=fresh, in0=partial[:], in1=factors[u == 1], op=MULT)
             nc.vector.tensor_copy(out=page[t][:].indirect(places[:, h * cols:(h + 1) * cols]), in_=fresh)
             if h == HALVES - 1:
                 nc.sync.dma_start(out=out_rows[t], in_=page[t][:])
         nc.scalar.activation(out=warm[:, 2:3], in_=damp[len(units) - 1][:, 0:1], func=ACT.Tanh)
-        rounded = reuse.tile([P, PACK, T2], BF16, name="rounded", offset=0)
+        rounded = keep.tile([P, PACK, T2], BF16, name="rounded", tag="size", align_bytes=64)
         for t in range(PACK - 1):
             nc.scalar.copy(out=rounded[:, t, :], in_=page[t][:])
 

@@ -46,11 +46,11 @@ def tile_list_rehab_embedding_refresh_kernel(
         tab_rows = held([P, T], U8, "tab_rows")
         nc.gpsimd.memset(tab_rows[:, T // 2:].bitcast(I32), 0)
         nc.vector.memset(tab_rows[:, :T // 2].bitcast(I32), 0)
-        w2_scale_raw = held([P, PASSES, H], U8, "w2_scale_raw")
-        nc.gpsimd.memset(w2_scale_raw[:].rearrange("p a c -> p (a c)").bitcast(I32), 0)
-        v_scale = [held([P, S], U8, f"v_scale{a}") for a in range(PASSES)]
+        w2_scale_raw = held([P, H], U8, "w2_scale_raw")
+        nc.gpsimd.memset(w2_scale_raw[:].bitcast(I32), 0)
+        planes = [held([P, S + H], U8, f"planes{a}") for a in range(PASSES)]
         for a in range(PASSES):
-            nc.vector.memset(v_scale[a][:].bitcast(I32), 0)
+            nc.vector.memset(planes[a][:].bitcast(I32), 0)
         w3_scale = held([P, N], U8, "w3_scale")
         nc.vector.memset(w3_scale[:].bitcast(I32), 0)
         warm = held([P, 3], F32, "warm")
@@ -71,18 +71,24 @@ def tile_list_rehab_embedding_refresh_kernel(
         nc.sync.dma_start(
             out=tab_rows[32:96:2, :].bitcast(I32), in_=tab_scales.bitcast(I32).rearrange("a q c -> (a q) c")
         )
-        w2_scale_rows = w2_scales.bitcast(I32).rearrange("a (Q r) c -> r Q a c", r=4)
-        for r in range(4):
-            nc.sync.dma_start(out=w2_scale_raw[r:P:32, :, :].bitcast(I32), in_=w2_scale_rows[r])
+        nc.sync.dma_start(
+            out=w2_scale_raw[32:96:2, :].bitcast(I32), in_=w2_scales.bitcast(I32).rearrange("a q c -> (a q) c")
+        )
 
         picked_rows = held([P, S], U8, "picked_rows")
         nc.vector.tensor_copy(out=picked_rows[:], in_=tab_rows[:].indirect(picks[:]))
+        staged = held([P, S + H], U8, "staged")
+        nc.vector.tensor_copy(
+            out=staged[:, S:].rearrange("p (t m) -> p t m", t=PACK),
+            in_=w2_scale_raw[:].rearrange("p (m t) -> p t m", t=PACK),
+        )
+        nc.vector.tensor_copy(out=staged[:, :S].bitcast(I32), in_=picked_rows[:].bitcast(I32))
 
         def place_scale_rows(a):
             for r in range(4):
                 nc.sync.dma_start(
-                    out=v_scale[a][r:P:32, :].bitcast(I32),
-                    in_=picked_rows[32 * a + 32 + 2 * r:32 * a + 64:8, :].bitcast(I32),
+                    out=planes[a][r:P:32, :].bitcast(I32),
+                    in_=staged[32 * a + 32 + 2 * r:32 * a + 64:8, :].bitcast(I32),
                 )
 
         load_table(0, slice(0, T))
@@ -129,11 +135,6 @@ def tile_list_rehab_embedding_refresh_kernel(
             out=w2[:].rearrange("p a (t m b) -> p a t m b", t=PACK, b=2),
             in_=w2_raw[:].rearrange("p a (m t b) -> p a t m b", t=PACK, b=2),
         )
-        w2_scale = held([P, PASSES, H], U8, "w2_scale")
-        nc.vector.tensor_copy(
-            out=w2_scale[:].rearrange("p a (t m) -> p a t m", t=PACK),
-            in_=w2_scale_raw[:].rearrange("p a (m t) -> p a t m", t=PACK),
-        )
 
         identity = held([P, P], F32, "identity")
         make_identity(nc, identity[:])
@@ -170,14 +171,14 @@ def tile_list_rehab_embedding_refresh_kernel(
                     lhsT=words[a][:, width * t * P:width * (t + 1) * P].bitcast(dtype),
                     lhsT_scale=scales[a][:, t * P:(t + 1) * P],
                     rhs=v[a][h][:].bitcast(FP8X4),
-                    rhs_scale=v_scale[a][:, h * BANK:(h + 1) * BANK],
+                    rhs_scale=planes[a][:, h * BANK:(h + 1) * BANK],
                     start=(a == 0),
                     stop=(a == PASSES - 1),
                 )
             return acc
 
         w2_passes = [w2[:, a, :] for a in range(PASSES)]
-        w2_scale_passes = [w2_scale[:, a, :] for a in range(PASSES)]
+        w2_scale_passes = [planes[a][:, S:] for a in range(PASSES)]
 
         units = [(t + i, h) for t in range(0, PACK, 2) for h in range(HALVES) for i in range(2)]
         size, damp = {}, {}

@@ -300,30 +300,51 @@ def tile_list_rehab_embedding_refresh_kernel(
             )
             nc.scalar.activation(out=out, in_=acc_c[:, :c1 - c0], func=ACT.Tanh, bias=bias[:, i:i + 1])
 
-        spans = (
-            (0, BANK, "features", (1, 2, 4, 6)),
-            (BANK, 2 * BANK, "tab1", (3, 6)),
-            (2 * BANK, T2, "tab0", (2, 4, 6)),
-        )
-        for s0, s1, space, ends in spans:
-            for c0 in range(s0, s1, BANK):
-                quantise(c0)
-            nc.sync.dma_start(out=code_rows[:, s0:s1], in_=codes[:, s0:s1].bitcast(I32))
-            if s1 == T2:
-                for quad in range(QUADS):
-                    nc.gpsimd.dma_start(
-                        out=scale_rows[4 * quad:4 * quad + 4, :],
-                        in_=scale[32 * quad:32 * quad + 4, :].bitcast(I32),
-                    )
-            result = keep.tile([P, N_TILES, s1 - s0], F32, name=f"features{s0}", tag=space, align_bytes=64)
-            early = 3 if s0 == 0 else 0
-            for i in range(early):
-                features(i, 0, BANK // 2, result[:, i, :BANK // 2])
-            stored = 0
-            for i in range(N_TILES):
-                for c0 in range(s0, s1, BANK):
-                    lo = BANK // 2 if i < early else c0
-                    features(i, lo, c0 + BANK, result[:, i, lo - s0:c0 - s0 + BANK])
-                if i + 1 in ends:
-                    nc.sync.dma_start(out=out_tiles[:, stored:i + 1, s0:s1], in_=result[:, stored:i + 1, :])
-                    stored = i + 1
+        for c0 in range(0, T2, BANK):
+            quantise(c0)
+        results = [
+            keep.tile([P, 2, T2], F32, name=f"features{i}", tag=space, align_bytes=64)
+            for i, space in enumerate(("features", "tab1", "tab0"))
+        ]
+
+        def make(i, c0, c1):
+            features(i, c0, c1, results[i // 2][:, i % 2, c0:c1])
+
+        def store(i0, i1, c0, c1):
+            nc.sync.dma_start(
+                out=out_tiles[:, i0:i1, c0:c1], in_=results[i0 // 2][:, i0 % 2:i0 % 2 + i1 - i0, c0:c1]
+            )
+
+        def store_codes(c0, c1):
+            nc.sync.dma_start(out=code_rows[:, c0:c1], in_=codes[:, c0:c1].bitcast(I32))
+
+        for i in range(2):
+            make(i, 0, BANK // 2)
+        store_codes(0, BANK)
+        for i in range(2):
+            make(i, BANK // 2, BANK)
+            store(i, i + 1, 0, BANK)
+        for i in range(2, 4):
+            make(i, 0, BANK)
+        store_codes(BANK, 2 * BANK)
+        for i in range(2, 4):
+            make(i, BANK, 2 * BANK)
+            store(i, i + 1, 0, 2 * BANK)
+        store_codes(2 * BANK, T2)
+        for quad in range(QUADS):
+            nc.gpsimd.dma_start(
+                out=scale_rows[4 * quad:4 * quad + 4, :], in_=scale[32 * quad:32 * quad + 4, :].bitcast(I32)
+            )
+        for i in range(4, N_TILES):
+            for c0 in (0, BANK):
+                make(i, c0, c0 + BANK)
+            store(i, i + 1, 0, 2 * BANK)
+        for i in range(2):
+            for c0 in range(BANK, T2, BANK):
+                make(i, c0, c0 + BANK)
+            store(i, i + 1, BANK, T2)
+        for i in range(2, N_TILES):
+            for c0 in (2 * BANK, 3 * BANK):
+                make(i, c0, c0 + BANK)
+            if i > 2:
+                store(2 if i == 3 else i, i + 1, 2 * BANK, T2)

@@ -35,6 +35,7 @@ def tile_list_rehab_embedding_refresh_kernel(
         keep = ctx.enter_context(tc.tile_pool(name="keep", bufs=1))
         ring = ctx.enter_context(tc.tile_pool(name="ring", bufs=2))
         reuse = ctx.enter_context(tc.tile_pool(name="reuse", bufs=1))
+        weaving = ctx.enter_context(tc.tile_pool(name="weaving", bufs=1))
         psum = ctx.enter_context(tc.psum_pool(name="psum", bufs=1))
 
         def held(shape, dtype, name):
@@ -262,26 +263,32 @@ def tile_list_rehab_embedding_refresh_kernel(
         scale_rows = out_3[0].bitcast(I32)
         code_rows = out_2[0].rearrange("p c i -> p (c i)").bitcast(I32)
 
-        def quantise(c0):
-            woven = ring.tile([P, BANK, PACK], BF16, name="woven", bufs=1, align_bytes=64)
-            if c0 == 0:
-                shares = ((nc.vector.tensor_copy, 0, BANK // 2), (nc.scalar.copy, BANK // 2, BANK))
-            else:
-                shares = ((nc.vector.tensor_copy, 0, BANK),)
-            for move, lo, hi in shares:
-                part = slice(c0 + lo, c0 + hi)
-                move(out=rounded[:, PACK - 1, part], in_=page[PACK - 1][:, part])
+        def weave(move, c0, c1, space):
+            woven = weaving.tile([P, c1 - c0, PACK], BF16, name=f"woven{c0}", offset=space, align_bytes=64)
+            move(out=rounded[:, PACK - 1, c0:c1], in_=page[PACK - 1][:, c0:c1])
+            step = BANK if c0 in (BANK, 3 * BANK) else BANK // 2
+            for lo in range(c0, c1, step):
                 move(
-                    out=woven[:, lo:hi, :].rearrange("p (c i) t -> p c t i", i=4),
-                    in_=rounded[:, :, part].rearrange("p t (c i) -> p c t i", i=4),
+                    out=woven[:, lo - c0:lo - c0 + step, :].rearrange("p (c i) t -> p c t i", i=4),
+                    in_=rounded[:, :, lo:lo + step].rearrange("p t (c i) -> p c t i", i=4),
                 )
-            for move, lo, hi in shares:
-                part = slice(c0 + lo, c0 + hi)
-                nc.vector.quantize_mx(
-                    out=codes[:, part].bitcast(FP8X4),
-                    scales=scale[:, part],
-                    in_=woven[:, lo:hi, :].rearrange("p c t -> p (c t)"),
-                )
+            return woven
+
+        def pack(woven, c0, c1):
+            nc.vector.quantize_mx(
+                out=codes[:, c0:c1].bitcast(FP8X4),
+                scales=scale[:, c0:c1],
+                in_=woven[:].rearrange("p c t -> p (c t)"),
+            )
+
+        def quantise(c0):
+            if c0 == 0:
+                halves = ((nc.vector.tensor_copy, 0, BANK // 2), (nc.scalar.copy, BANK // 2, BANK))
+                woven = [weave(move, lo, hi, (8192, 3072)[i]) for i, (move, lo, hi) in enumerate(halves)]
+                for i, (move, lo, hi) in enumerate(halves):
+                    pack(woven[i], lo, hi)
+            else:
+                pack(weave(nc.vector.tensor_copy, c0, c0 + BANK, 4096 * ((c0 // BANK + 1) % 2)), c0, c0 + BANK)
 
         banks = list(range(8)) * 4
         out_tiles = out_0.rearrange("(i p) c -> p i c", p=P)
@@ -302,49 +309,43 @@ def tile_list_rehab_embedding_refresh_kernel(
 
         for c0 in range(0, T2, BANK):
             quantise(c0)
-        results = [
-            keep.tile([P, 2, T2], F32, name=f"features{i}", tag=space, align_bytes=64)
-            for i, space in enumerate(("features", "tab1", "tab0"))
-        ]
+        spaces = ("features", "tab1", "tab0")
+        results = [keep.tile([P, 2 * T2], F32, name=f"features{i}", tag=spaces[i], align_bytes=64) for i in range(3)]
 
         def make(i, c0, c1):
-            features(i, c0, c1, results[i // 2][:, i % 2, c0:c1])
+            features(i, c0, c1, results[i // 2][:, i % 2 * T2 + c0:i % 2 * T2 + c1])
 
-        def store(i0, i1, c0, c1):
-            nc.sync.dma_start(
-                out=out_tiles[:, i0:i1, c0:c1], in_=results[i0 // 2][:, i0 % 2:i0 % 2 + i1 - i0, c0:c1]
-            )
+        def store(i, c0, c1):
+            nc.sync.dma_start(out=out_tiles[:, i, c0:c1], in_=results[i // 2][:, i % 2 * T2 + c0:i % 2 * T2 + c1])
 
         def store_codes(c0, c1):
             nc.sync.dma_start(out=code_rows[:, c0:c1], in_=codes[:, c0:c1].bitcast(I32))
 
-        for i in range(2):
-            make(i, 0, BANK // 2)
+        lead, early = 4, 3
+        first = held([P, lead, BANK], F32, "first_span")
+        for i in range(early):
+            features(i, 0, BANK // 2, first[:, i, :BANK // 2])
         store_codes(0, BANK)
-        for i in range(2):
-            make(i, BANK // 2, BANK)
-            store(i, i + 1, 0, BANK)
-        for i in range(2, 4):
-            make(i, 0, BANK)
+        stored = 0
+        for i in range(lead):
+            lo = BANK // 2 if i < early else 0
+            features(i, lo, BANK, first[:, i, lo:])
+            if i != 2:
+                nc.sync.dma_start(out=out_tiles[:, stored:i + 1, :BANK], in_=first[:, stored:i + 1, :])
+                stored = i + 1
         store_codes(BANK, 2 * BANK)
-        for i in range(2, 4):
-            make(i, BANK, 2 * BANK)
-            store(i, i + 1, 0, 2 * BANK)
-        store_codes(2 * BANK, T2)
+        for i in range(lead, N_TILES):
+            for c0 in (0, BANK):
+                make(i, c0, c0 + BANK)
+            store(i, 0, 2 * BANK)
+        store_codes(2 * BANK, 3 * BANK)
+        store_codes(3 * BANK, T2)
         for quad in range(QUADS):
             nc.gpsimd.dma_start(
                 out=scale_rows[4 * quad:4 * quad + 4, :], in_=scale[32 * quad:32 * quad + 4, :].bitcast(I32)
             )
-        for i in range(4, N_TILES):
-            for c0 in (0, BANK):
+        for i in range(N_TILES):
+            start = BANK if i < lead else 2 * BANK
+            for c0 in range(start, T2, BANK):
                 make(i, c0, c0 + BANK)
-            store(i, i + 1, 0, 2 * BANK)
-        for i in range(2):
-            for c0 in range(BANK, T2, BANK):
-                make(i, c0, c0 + BANK)
-            store(i, i + 1, BANK, T2)
-        for i in range(2, N_TILES):
-            for c0 in (2 * BANK, 3 * BANK):
-                make(i, c0, c0 + BANK)
-            if i > 2:
-                store(2 if i == 3 else i, i + 1, 2 * BANK, T2)
+            store(i, start, T2)

@@ -338,8 +338,7 @@ def tile_list_rehab_embedding_refresh_kernel(
             for c0 in (0, BANK):
                 make(i, c0, c0 + BANK)
             store(i, 0, 2 * BANK)
-        store_codes(2 * BANK, 3 * BANK)
-        store_codes(3 * BANK, T2)
+        store_codes(2 * BANK, T2)
         for quad in range(QUADS):
             nc.gpsimd.dma_start(
                 out=scale_rows[4 * quad:4 * quad + 4, :], in_=scale[32 * quad:32 * quad + 4, :].bitcast(I32)

@@ -16,6 +16,7 @@ FP8X4 = mybir.dt.float8_e4m3fn_x4
 FP4X4 = mybir.dt.float4_e2m1fn_x4
 ACT = mybir.ActivationFunctionType
 MULT = mybir.AluOpType.mult
+ADD = mybir.AluOpType.add
 
 P = 128
 PACK = 4
@@ -254,41 +255,50 @@ def tile_list_rehab_embedding_refresh_kernel(
             if h == HALVES - 1:
                 nc.sync.dma_start(out=out_rows[t], in_=page[t][:])
         nc.scalar.activation(out=warm[:, 2:3], in_=damp[len(units) - 1][:, 0:1], func=ACT.Tanh)
-        rounded = keep.tile([P, PACK, T2], BF16, name="rounded", tag="size", align_bytes=64)
-        for t in range(PACK - 1):
-            nc.scalar.copy(out=rounded[:, t, :], in_=page[t][:])
+        half = T2 // 2
+        spans = ((0, BANK // 2), (BANK // 2, BANK), (BANK, half))
+        pairs = keep.tile([P, 2 * half], F32, name="pairs", tag="size", align_bytes=64)
+        rounded = ring.tile([P, PACK, half], BF16, name="rounded", tag="partial", bufs=1)
+
+        def pair_words(c0, c1):
+            return pairs[:, 2 * c0:2 * c1].rearrange("p (u c) -> p u c", u=2)
+
+        def round_into_pairs(t, c0, c1):
+            halves = pairs[:, 2 * c0:2 * c1].bitcast(BF16).rearrange("p (u c e) -> p u e c", u=2, e=2)
+            nc.scalar.copy(out=halves[:, t // 2, t % 2, :], in_=page[t][:, c0:c1])
+
+        for t in range(2):
+            for c0, c1 in spans:
+                round_into_pairs(t, c0, c1)
+            nc.gpsimd.tensor_scalar(
+                out=rounded[:, t, :], in0=page[t][:, half:], scalar1=1.0, scalar2=-0.0, op0=MULT, op1=ADD
+            )
+        for c0, c1 in spans:
+            round_into_pairs(2, c0, c1)
+        nc.scalar.copy(out=rounded[:, 2, :], in_=page[2][:, half:])
+        for c0, c1 in spans:
+            round_into_pairs(3, c0, c1)
 
         codes = held([P, T2], U32, "codes")
         scale = held([P, T2], U8, "scale")
         scale_rows = out_3[0].bitcast(I32)
         code_rows = out_2[0].rearrange("p c i -> p (c i)").bitcast(I32)
 
-        def weave(move, c0, c1, space):
-            woven = weaving.tile([P, c1 - c0, PACK], BF16, name=f"woven{c0}", offset=space, align_bytes=64)
-            move(out=rounded[:, PACK - 1, c0:c1], in_=page[PACK - 1][:, c0:c1])
-            step = BANK if c0 in (BANK, 3 * BANK) else BANK // 2
-            for lo in range(c0, c1, step):
-                move(
-                    out=woven[:, lo - c0:lo - c0 + step, :].rearrange("p (c i) t -> p c t i", i=4),
-                    in_=rounded[:, :, lo:lo + step].rearrange("p t (c i) -> p c t i", i=4),
-                )
-            return woven
-
         def pack(woven, c0, c1):
-            nc.vector.quantize_mx(
-                out=codes[:, c0:c1].bitcast(FP8X4),
-                scales=scale[:, c0:c1],
-                in_=woven[:].rearrange("p c t -> p (c t)"),
-            )
+            nc.vector.quantize_mx(out=codes[:, c0:c1].bitcast(FP8X4), scales=scale[:, c0:c1], in_=woven)
 
-        def quantise(c0):
-            if c0 == 0:
-                halves = ((nc.vector.tensor_copy, 0, BANK // 2), (nc.scalar.copy, BANK // 2, BANK))
-                woven = [weave(move, lo, hi, (8192, 3072)[i]) for i, (move, lo, hi) in enumerate(halves)]
-                for i, (move, lo, hi) in enumerate(halves):
-                    pack(woven[i], lo, hi)
-            else:
-                pack(weave(nc.vector.tensor_copy, c0, c0 + BANK, 4096 * ((c0 // BANK + 1) % 2)), c0, c0 + BANK)
+        for c0, c1 in spans:
+            woven = weaving.tile([P, c1 - c0, 2], F32, name=f"woven{c0}", offset=8 * min(c0, BANK // 2), align_bytes=64)
+            nc.vector.tensor_copy(out=woven[:], in_=pair_words(c0, c1).rearrange("p u c -> p c u"))
+            pack(woven[:].rearrange("p c u -> p (c u)").bitcast(BF16), c0, c1)
+        for c0 in range(0, half, BANK):
+            woven = weaving.tile([P, BANK, PACK], BF16, name=f"late{c0}", offset=8 * c0, align_bytes=64)
+            nc.vector.tensor_copy(out=rounded[:, 3, c0:c0 + BANK], in_=page[3][:, half + c0:half + c0 + BANK])
+            nc.vector.tensor_copy(
+                out=woven[:].rearrange("p (c i) t -> p c t i", i=4),
+                in_=rounded[:, :, c0:c0 + BANK].rearrange("p t (c i) -> p c t i", i=4),
+            )
+            pack(woven[:].rearrange("p c t -> p (c t)"), half + c0, half + c0 + BANK)
 
         banks = list(range(8)) * 4
         out_tiles = out_0.rearrange("(i p) c -> p i c", p=P)
@@ -307,8 +317,6 @@ def tile_list_rehab_embedding_refresh_kernel(
             )
             nc.scalar.activation(out=out, in_=acc_c[:, :c1 - c0], func=ACT.Tanh, bias=bias[:, i:i + 1])
 
-        for c0 in range(0, T2, BANK):
-            quantise(c0)
         spaces = ("features", "tab1", "tab0")
         results = [keep.tile([P, 2 * T2], F32, name=f"features{i}", tag=spaces[i], align_bytes=64) for i in range(3)]
 
@@ -321,30 +329,24 @@ def tile_list_rehab_embedding_refresh_kernel(
         def store_codes(c0, c1):
             nc.sync.dma_start(out=code_rows[:, c0:c1], in_=codes[:, c0:c1].bitcast(I32))
 
-        lead, early = 4, 3
-        first = held([P, lead, BANK], F32, "first_span")
-        for i in range(early):
-            features(i, 0, BANK // 2, first[:, i, :BANK // 2])
+        for c0, c1 in spans[:2]:
+            for i in range(2):
+                make(i, c0, c1)
         store_codes(0, BANK)
-        stored = 0
-        for i in range(lead):
-            lo = BANK // 2 if i < early else 0
-            features(i, lo, BANK, first[:, i, lo:])
-            if i != 2:
-                nc.sync.dma_start(out=out_tiles[:, stored:i + 1, :BANK], in_=first[:, stored:i + 1, :])
-                stored = i + 1
-        store_codes(BANK, 2 * BANK)
-        for i in range(lead, N_TILES):
-            for c0 in (0, BANK):
+        make(2, 0, BANK)
+        for i in range(3):
+            store(i, 0, BANK)
+        store_codes(BANK, half)
+        for i in range(3, N_TILES - 1):
+            for c0 in range(0, half, BANK):
                 make(i, c0, c0 + BANK)
-            store(i, 0, 2 * BANK)
-        store_codes(2 * BANK, T2)
+            store(i, 0, half)
+        store_codes(half, T2)
         for quad in range(QUADS):
             nc.gpsimd.dma_start(
                 out=scale_rows[4 * quad:4 * quad + 4, :], in_=scale[32 * quad:32 * quad + 4, :].bitcast(I32)
             )
-        for i in range(N_TILES):
-            start = BANK if i < lead else 2 * BANK
+        for i, start in ((5, 0), (0, BANK), (1, BANK), (2, BANK), (3, half), (4, half)):
             for c0 in range(start, T2, BANK):
                 make(i, c0, c0 + BANK)
             store(i, start, T2)

@@ -46,10 +46,9 @@ def tile_list_rehab_embedding_refresh_kernel(
         places = keep.tile([P, S // 16], U16, name="places")
 
         tab_rows = held([P, T], U8, "tab_rows")
-        nc.gpsimd.memset(tab_rows[:, T // 2:].bitcast(I32), 0)
-        nc.vector.memset(tab_rows[:, :T // 2].bitcast(I32), 0)
+        nc.vector.memset(tab_rows[:].bitcast(I32), 0)
         w2_scale_raw = held([P, H], U8, "w2_scale_raw")
-        nc.gpsimd.memset(w2_scale_raw[:].bitcast(I32), 0)
+        nc.vector.memset(w2_scale_raw[:].bitcast(I32), 0)
         planes = [held([P, S + H], U8, f"planes{a}") for a in range(PASSES)]
         for a in range(PASSES):
             nc.vector.memset(planes[a][:].bitcast(I32), 0)

@@ -45,13 +45,13 @@ def tile_list_rehab_embedding_refresh_kernel(
         picks = keep.tile([P, S // 16], U16, name="picks")
         places = keep.tile([P, S // 16], U16, name="places")
 
-        tab_rows = held([P, T], U8, "tab_rows")
-        nc.vector.memset(tab_rows[:].bitcast(I32), 0)
-        w2_scale_raw = held([P, H], U8, "w2_scale_raw")
-        nc.vector.memset(w2_scale_raw[:].bitcast(I32), 0)
-        planes = [held([P, S + H], U8, f"planes{a}") for a in range(PASSES)]
-        for a in range(PASSES):
-            nc.vector.memset(planes[a][:].bitcast(I32), 0)
+        tab_rows = [held([P, T], U8, f"tab_rows{a}") for a in range(PASSES)]
+        w2_rows = held([P, PASSES, H], U8, "w2_rows")
+        nc.vector.memset(w2_rows[:].bitcast(I32), 0)
+        nc.vector.memset(tab_rows[0][:].bitcast(I32), 0)
+        nc.gpsimd.memset(tab_rows[1][:].bitcast(I32), 0)
+        planes = held([P, PASSES * (S + H)], U8, "planes")
+        nc.vector.memset(planes[:].bitcast(I32), 0)
         w3_scale = held([P, N], U8, "w3_scale")
         nc.vector.memset(w3_scale[:].bitcast(I32), 0)
         warm = held([P, 3], F32, "warm")
@@ -60,43 +60,36 @@ def tile_list_rehab_embedding_refresh_kernel(
 
         tab = [held([P, T], U32, f"tab{a}") for a in range(PASSES)]
 
-        def load_table(a, part):
+        def load_table(a):
             words = tab_words[a].rearrange("p t i -> p (t i)").bitcast(I32)
-            nc.sync.dma_start(out=tab[a][:, part].bitcast(I32), in_=words[:, part])
+            nc.sync.dma_start(out=tab[a][:].bitcast(I32), in_=words)
 
         nc.sync.dma_start(picks[:], offs)
         gain_head = held([P, BANK], F32, "gain_head")
         nc.sync.dma_start(out=gain_head[:], in_=wgs[:, :BANK])
         w2_raw = held([P, PASSES, 2 * H], U8, "w2_raw")
         nc.sync.dma_start(out=w2_raw[:].bitcast(I32), in_=w2_words.bitcast(I32).rearrange("a p c -> p a c"))
+        nc.sync.dma_start(places[:], offs2)
         nc.sync.dma_start(
-            out=tab_rows[32:96:2, :].bitcast(I32), in_=tab_scales.bitcast(I32).rearrange("a q c -> (a q) c")
+            out=w2_rows[32:96:4].bitcast(I32), in_=w2_scales.bitcast(I32).rearrange("a q c -> q a c")
         )
-        nc.sync.dma_start(
-            out=w2_scale_raw[32:96:2, :].bitcast(I32), in_=w2_scales.bitcast(I32).rearrange("a q c -> (a q) c")
-        )
+        for a in range(PASSES):
+            nc.sync.dma_start(out=tab_rows[a][32:96:4, :].bitcast(I32), in_=tab_scales[a].bitcast(I32))
 
-        picked_rows = held([P, S], U8, "picked_rows")
-        nc.vector.tensor_copy(out=picked_rows[:], in_=tab_rows[:].indirect(picks[:]))
-        staged = held([P, S + H], U8, "staged")
+        staged = held([P, PASSES * (S + H)], U8, "staged")
         nc.vector.tensor_copy(
-            out=staged[:, S:].rearrange("p (t m) -> p t m", t=PACK),
-            in_=w2_scale_raw[:].rearrange("p (m t) -> p t m", t=PACK),
+            out=staged[:, PASSES * S:].rearrange("p (a t m) -> p a t m", a=PASSES, t=PACK),
+            in_=w2_rows[:].rearrange("p a (m t) -> p a t m", t=PACK),
         )
-        nc.vector.tensor_copy(out=staged[:, :S].bitcast(I32), in_=picked_rows[:].bitcast(I32))
+        picked = reuse.tile([P, PASSES * S], U8, name="picked", offset=9 * 1024, align_bytes=64)
+        for a in range(PASSES):
+            nc.vector.tensor_copy(out=picked[:, a * S:(a + 1) * S], in_=tab_rows[a][:].indirect(picks[:]))
+        nc.vector.tensor_copy(out=staged[:, :PASSES * S].bitcast(I32), in_=picked[:].bitcast(I32))
 
-        def place_scale_rows(a):
-            for r in range(4):
-                nc.sync.dma_start(
-                    out=planes[a][r:P:32, :].bitcast(I32),
-                    in_=staged[32 * a + 32 + 2 * r:32 * a + 64:8, :].bitcast(I32),
-                )
-
-        load_table(0, slice(0, T))
-        load_table(1, slice(0, T // 2))
-        place_scale_rows(0)
-        load_table(1, slice(T // 2, T))
-        place_scale_rows(1)
+        load_table(0)
+        load_table(1)
+        for r in range(4):
+            nc.sync.dma_start(out=planes[r:P:32, :].bitcast(I32), in_=staged[32 + 4 * r:96:16, :].bitcast(I32))
 
         w1_raw = [held([P, PACK, H], F32, "w1_raw0"), reuse.tile([P, PACK, H], F32, name="w1_raw1", offset=0)]
         w1_rows = w1.rearrange("(a p j) c -> a p j c", a=PASSES, j=PACK)
@@ -114,7 +107,6 @@ def tile_list_rehab_embedding_refresh_kernel(
         page_rows = page0.rearrange("(p t) c -> t p c", t=PACK)
         nc.sync.dma_start(out=w1_raw[0][:], in_=w1_rows[0])
         nc.sync.dma_start(out=w1_raw[1][:], in_=w1_rows[1])
-        nc.sync.dma_start(places[:], offs2)
         for t in range(0, PACK, 2):
             for i in range(2):
                 nc.sync.dma_start(out=page[t + i][:], in_=page_rows[t + i])
@@ -132,9 +124,9 @@ def tile_list_rehab_embedding_refresh_kernel(
             nc.sync.dma_start(out=bias[:], in_=b3.rearrange("(i p) -> p i", p=P))
 
         w2 = held([P, PASSES, 2 * H], U8, "w2")
-        nc.vector.tensor_copy(
-            out=w2[:].rearrange("p a (t m b) -> p a t m b", t=PACK, b=2),
-            in_=w2_raw[:].rearrange("p a (m t b) -> p a t m b", t=PACK, b=2),
+        nc.scalar.copy(
+            out=w2[:].bitcast(U16).rearrange("p a (t m) -> p a m t", t=PACK),
+            in_=w2_raw[:].bitcast(U16).rearrange("p a (m t) -> p a m t", t=PACK),
         )
 
         identity = held([P, P], F32, "identity")
@@ -157,7 +149,10 @@ def tile_list_rehab_embedding_refresh_kernel(
             nc.scalar.copy(out=gain[0][:, t * BANK:(t + 1) * BANK], in_=back[:])
 
         cols = BANK // 16
-        v = [[held([P, BANK], U32, f"v{a}_{h}") for h in range(HALVES)] for a in range(PASSES)]
+        v = [
+            [reuse.tile([P, BANK], U32, name=f"v0_{h}", offset=(8 + 2 * h) * 1024, align_bytes=64) for h in range(HALVES)],
+            [held([P, BANK], U32, f"v1_{h}") for h in range(HALVES)],
+        ]
         for a in range(PASSES):
             for h in range(HALVES):
                 nc.vector.tensor_copy(
@@ -172,14 +167,14 @@ def tile_list_rehab_embedding_refresh_kernel(
                     lhsT=words[a][:, width * t * P:width * (t + 1) * P].bitcast(dtype),
                     lhsT_scale=scales[a][:, t * P:(t + 1) * P],
                     rhs=v[a][h][:].bitcast(FP8X4),
-                    rhs_scale=planes[a][:, h * BANK:(h + 1) * BANK],
+                    rhs_scale=planes[:, a * S + h * BANK:a * S + (h + 1) * BANK],
                     start=(a == 0),
                     stop=(a == PASSES - 1),
                 )
             return acc
 
         w2_passes = [w2[:, a, :] for a in range(PASSES)]
-        w2_scale_passes = [planes[a][:, S:] for a in range(PASSES)]
+        w2_scale_passes = [planes[:, PASSES * S + a * H:PASSES * S + (a + 1) * H] for a in range(PASSES)]
 
         units = [(t + i, h) for t in range(0, PACK, 2) for h in range(HALVES) for i in range(2)]
         size, damp = {}, {}
@@ -214,8 +209,9 @@ def tile_list_rehab_embedding_refresh_kernel(
             if a == 0:
                 nc.vector.tensor_copy(out=dst, in_=src)
             else:
-                nc.vector.tensor_copy(out=dst[:, :96], in_=src[:, :96])
-                nc.scalar.copy(out=dst[:, 96:], in_=src[:, 96:])
+                nc.vector.tensor_copy(out=dst[:, :, :, :2], in_=src[:, :, :, :2])
+                nc.vector.tensor_copy(out=dst[:, :64, :, 2:], in_=src[:, :64, :, 2:])
+                nc.scalar.copy(out=dst[:, 64:, :, 2:], in_=src[:, 64:, :, 2:])
                 inverse_root(1)
             for c0, c1 in ((0, H),) if a == 0 else ((0, P), (P, 2 * P), (2 * P, H)):
                 nc.vector.quantize_mx(
@@ -235,8 +231,8 @@ def tile_list_rehab_embedding_refresh_kernel(
             else:
                 raw = ring.tile([P, BANK], F32, name="raw", bufs=4)
                 if u == 1:
-                    squared(u)
                     nc.scalar.copy(out=raw[:], in_=acc_a[:])
+                    squared(u)
                     size_of_b(u + 1)
                     inverse_root(u + 1)
                 else:
@@ -247,8 +243,8 @@ def tile_list_rehab_embedding_refresh_kernel(
                         inverse_root(u + 1)
                     nc.scalar.copy(out=raw[:], in_=acc_a[:])
                 partial = ring.tile([P, BANK], F32, name="partial", bufs=1)
-                factors = (gain[h][:, t * BANK:(t + 1) * BANK], raw[:])
-                nc.gpsimd.tensor_tensor(out=partial[:], in0=damp[u][:], in1=factors[u != 1], op=MULT)
+                factors = (gain[h][:, t * BANK:(t + 1) * BANK], damp[u][:])
+                nc.gpsimd.tensor_tensor(out=partial[:], in0=raw[:], in1=factors[u != 1], op=MULT)
                 nc.gpsimd.tensor_tensor(out=fresh, in0=partial[:], in1=factors[u == 1], op=MULT)
             nc.vector.tensor_copy(out=page[t][:].indirect(places[:, h * cols:(h + 1) * cols]), in_=fresh)
             if h == HALVES - 1:

@@ -50,8 +50,10 @@ def tile_list_rehab_embedding_refresh_kernel(
         nc.vector.memset(w2_rows[:].bitcast(I32), 0)
         nc.vector.memset(tab_rows[0][:].bitcast(I32), 0)
         nc.gpsimd.memset(tab_rows[1][:].bitcast(I32), 0)
-        planes = held([P, PASSES * (S + H)], U8, "planes")
-        nc.vector.memset(planes[:].bitcast(I32), 0)
+        group = PASSES * (S + H) // HALVES
+        planes = [held([P, group], U8, f"planes{h}") for h in range(HALVES)]
+        for h in range(HALVES):
+            nc.vector.memset(planes[h][:].bitcast(I32), 0)
         w3_scale = held([P, N], U8, "w3_scale")
         nc.vector.memset(w3_scale[:].bitcast(I32), 0)
         warm = held([P, 3], F32, "warm")
@@ -76,20 +78,33 @@ def tile_list_rehab_embedding_refresh_kernel(
         for a in range(PASSES):
             nc.sync.dma_start(out=tab_rows[a][32:96:4, :].bitcast(I32), in_=tab_scales[a].bitcast(I32))
 
-        staged = held([P, PASSES * (S + H)], U8, "staged")
-        nc.vector.tensor_copy(
-            out=staged[:, PASSES * S:].rearrange("p (a t m) -> p a t m", a=PASSES, t=PACK),
-            in_=w2_rows[:].rearrange("p a (m t) -> p a t m", t=PACK),
-        )
+        staged = [held([P, group], U8, f"staged{h}") for h in range(HALVES)]
+        for h in range(HALVES):
+            nc.vector.tensor_copy(
+                out=staged[h][:, S:].rearrange("p (a t m) -> p a t m", a=PASSES, t=2),
+                in_=w2_rows[:].rearrange("p a (m t) -> p a t m", t=PACK)[:, :, 2 * h:2 * h + 2, :],
+            )
         picked = reuse.tile([P, PASSES * S], U8, name="picked", offset=9 * 1024, align_bytes=64)
-        for a in range(PASSES):
-            nc.vector.tensor_copy(out=picked[:, a * S:(a + 1) * S], in_=tab_rows[a][:].indirect(picks[:]))
-        nc.vector.tensor_copy(out=staged[:, :PASSES * S].bitcast(I32), in_=picked[:].bitcast(I32))
+        cols = BANK // 16
+        for h in range(HALVES):
+            for a in range(PASSES):
+                nc.vector.tensor_copy(
+                    out=picked[:, h * S + a * BANK:h * S + (a + 1) * BANK],
+                    in_=tab_rows[a][:].indirect(picks[:, h * cols:(h + 1) * cols]),
+                )
+            nc.vector.tensor_copy(
+                out=staged[h][:, :S].bitcast(I32), in_=picked[:, h * S:(h + 1) * S].bitcast(I32)
+            )
+
+        def move_scale_rows(h):
+            for r in range(4):
+                nc.sync.dma_start(
+                    out=planes[h][r:P:32, :].bitcast(I32), in_=staged[h][32 + 4 * r:96:16, :].bitcast(I32)
+                )
 
         load_table(0)
         load_table(1)
-        for r in range(4):
-            nc.sync.dma_start(out=planes[r:P:32, :].bitcast(I32), in_=staged[32 + 4 * r:96:16, :].bitcast(I32))
+        move_scale_rows(0)
 
         w1_raw = [held([P, PACK, H], F32, "w1_raw0"), reuse.tile([P, PACK, H], F32, name="w1_raw1", offset=0)]
         w1_rows = w1.rearrange("(a p j) c -> a p j c", a=PASSES, j=PACK)
@@ -110,6 +125,8 @@ def tile_list_rehab_embedding_refresh_kernel(
         for t in range(0, PACK, 2):
             for i in range(2):
                 nc.sync.dma_start(out=page[t + i][:], in_=page_rows[t + i])
+                if t + i == 0:
+                    move_scale_rows(1)
             for i in range(2):
                 load_gain(t + i)
         w3 = held([P, N], U32, "w3")
@@ -148,7 +165,6 @@ def tile_list_rehab_embedding_refresh_kernel(
                 nc.tensor.transpose(back[:, block], dealt[:, j, t, :], identity[:])
             nc.scalar.copy(out=gain[0][:, t * BANK:(t + 1) * BANK], in_=back[:])
 
-        cols = BANK // 16
         v = [
             [reuse.tile([P, BANK], U32, name=f"v0_{h}", offset=(8 + 2 * h) * 1024, align_bytes=64) for h in range(HALVES)],
             [held([P, BANK], U32, f"v1_{h}") for h in range(HALVES)],
@@ -165,22 +181,28 @@ def tile_list_rehab_embedding_refresh_kernel(
                 nc.tensor.matmul_mx(
                     out=acc[:],
                     lhsT=words[a][:, width * t * P:width * (t + 1) * P].bitcast(dtype),
-                    lhsT_scale=scales[a][:, t * P:(t + 1) * P],
+                    lhsT_scale=scales(a, t),
                     rhs=v[a][h][:].bitcast(FP8X4),
-                    rhs_scale=planes[:, a * S + h * BANK:a * S + (h + 1) * BANK],
+                    rhs_scale=planes[h][:, a * BANK:(a + 1) * BANK],
                     start=(a == 0),
                     stop=(a == PASSES - 1),
                 )
             return acc
 
         w2_passes = [w2[:, a, :] for a in range(PASSES)]
-        w2_scale_passes = [planes[:, PASSES * S + a * H:PASSES * S + (a + 1) * H] for a in range(PASSES)]
+
+        def w2_scale_of(a, t):
+            first = S + (2 * a + t % 2) * P
+            return planes[t // 2][:, first:first + P]
+
+        def w1_scale_of(a, t):
+            return w1_scale[a][:, t * P:(t + 1) * P]
 
         units = [(t + i, h) for t in range(0, PACK, 2) for h in range(HALVES) for i in range(2)]
         size, damp = {}, {}
 
         def size_of_b(u):
-            acc_b = product(w2_passes, w2_scale_passes, FP4X4, 2, *units[u], u % 5)
+            acc_b = product(w2_passes, w2_scale_of, FP4X4, 2, *units[u], u % 5)
             size[u] = held([P, BANK], F32, "size")
             nc.scalar.activation(out=size[u][:], in_=acc_b[:], func=ACT.Abs)
 
@@ -225,7 +247,7 @@ def tile_list_rehab_embedding_refresh_kernel(
         out_rows = out_1.rearrange("(p t) c -> t p c", t=PACK)
         for u, (t, h) in enumerate(units):
             fresh = held([P, BANK], F32, f"fresh{u}")[:]
-            acc_a = product(w1_codes, w1_scale, FP8X4, 1, t, h, (u + 3) % 5)
+            acc_a = product(w1_codes, w1_scale_of, FP8X4, 1, t, h, (u + 3) % 5)
             if u == 0:
                 nc.vector.tensor_tensor(out=fresh, in0=acc_a[:], in1=first_factor[:], op=MULT)
             else:

@@ -50,8 +50,7 @@ def tile_list_rehab_embedding_refresh_kernel(
         nc.vector.memset(w2_rows[:].bitcast(I32), 0)
         nc.vector.memset(tab_rows[0][:].bitcast(I32), 0)
         nc.gpsimd.memset(tab_rows[1][:].bitcast(I32), 0)
-        group = PASSES * (S + H) // HALVES
-        planes = [held([P, group], U8, f"planes{h}") for h in range(HALVES)]
+        planes = [held([P, S + PASSES * H], U8, "planes0"), held([P, S], U8, "planes1")]
         for h in range(HALVES):
             nc.vector.memset(planes[h][:].bitcast(I32), 0)
         w3_scale = held([P, N], U8, "w3_scale")
@@ -69,37 +68,38 @@ def tile_list_rehab_embedding_refresh_kernel(
         nc.sync.dma_start(picks[:], offs)
         gain_head = held([P, BANK], F32, "gain_head")
         nc.sync.dma_start(out=gain_head[:], in_=wgs[:, :BANK])
-        w2_raw = held([P, PASSES, 2 * H], U8, "w2_raw")
-        nc.sync.dma_start(out=w2_raw[:].bitcast(I32), in_=w2_words.bitcast(I32).rearrange("a p c -> p a c"))
-        nc.sync.dma_start(places[:], offs2)
         nc.sync.dma_start(
             out=w2_rows[32:96:4].bitcast(I32), in_=w2_scales.bitcast(I32).rearrange("a q c -> q a c")
         )
+        w2_raw = held([P, PASSES, 2 * H], U8, "w2_raw")
+        nc.sync.dma_start(out=w2_raw[:].bitcast(I32), in_=w2_words.bitcast(I32).rearrange("a p c -> p a c"))
+        nc.sync.dma_start(places[:], offs2)
         for a in range(PASSES):
             nc.sync.dma_start(out=tab_rows[a][32:96:4, :].bitcast(I32), in_=tab_scales[a].bitcast(I32))
 
-        staged = [held([P, group], U8, f"staged{h}") for h in range(HALVES)]
-        for h in range(HALVES):
-            nc.vector.tensor_copy(
-                out=staged[h][:, S:].rearrange("p (a t m) -> p a t m", a=PASSES, t=2),
-                in_=w2_rows[:].rearrange("p a (m t) -> p a t m", t=PACK)[:, :, 2 * h:2 * h + 2, :],
-            )
-        picked = reuse.tile([P, PASSES * S], U8, name="picked", offset=9 * 1024, align_bytes=64)
+        staged = held([P, S + PASSES * H], U8, "staged")
+        nc.vector.tensor_copy(
+            out=staged[:, S:].rearrange("p (a t m) -> p a t m", a=PASSES, t=PACK),
+            in_=w2_rows[:].rearrange("p a (m t) -> p a t m", t=PACK),
+        )
+        picked = [
+            reuse.tile([P, S], U8, name="picked0", offset=9 * 1024 + BANK, align_bytes=64),
+            held([P, S], U8, "picked1"),
+        ]
         cols = BANK // 16
         for h in range(HALVES):
             for a in range(PASSES):
                 nc.vector.tensor_copy(
-                    out=picked[:, h * S + a * BANK:h * S + (a + 1) * BANK],
+                    out=picked[h][:, a * BANK:(a + 1) * BANK],
                     in_=tab_rows[a][:].indirect(picks[:, h * cols:(h + 1) * cols]),
                 )
-            nc.vector.tensor_copy(
-                out=staged[h][:, :S].bitcast(I32), in_=picked[:, h * S:(h + 1) * S].bitcast(I32)
-            )
+            if h == 0:
+                nc.vector.tensor_copy(out=staged[:, :S].bitcast(I32), in_=picked[0][:].bitcast(I32))
 
         def move_scale_rows(h):
             for r in range(4):
                 nc.sync.dma_start(
-                    out=planes[h][r:P:32, :].bitcast(I32), in_=staged[h][32 + 4 * r:96:16, :].bitcast(I32)
+                    out=planes[h][r:P:32, :].bitcast(I32), in_=(staged, picked[1])[h][32 + 4 * r:96:16, :].bitcast(I32)
                 )
 
         load_table(0)
@@ -122,13 +122,12 @@ def tile_list_rehab_embedding_refresh_kernel(
         page_rows = page0.rearrange("(p t) c -> t p c", t=PACK)
         nc.sync.dma_start(out=w1_raw[0][:], in_=w1_rows[0])
         nc.sync.dma_start(out=w1_raw[1][:], in_=w1_rows[1])
-        for t in range(0, PACK, 2):
-            for i in range(2):
-                nc.sync.dma_start(out=page[t + i][:], in_=page_rows[t + i])
-                if t + i == 0:
-                    move_scale_rows(1)
-            for i in range(2):
-                load_gain(t + i)
+        for t in range(PACK):
+            nc.sync.dma_start(out=page[t][:], in_=page_rows[t])
+            if t == 1:
+                move_scale_rows(1)
+        for t in range(PACK):
+            load_gain(t)
         w3 = held([P, N], U32, "w3")
         nc.sync.dma_start(
             out=w3[:].bitcast(I32), in_=w3_words[0].rearrange("p c i -> p (c i)").bitcast(I32)
@@ -192,13 +191,13 @@ def tile_list_rehab_embedding_refresh_kernel(
         w2_passes = [w2[:, a, :] for a in range(PASSES)]
 
         def w2_scale_of(a, t):
-            first = S + (2 * a + t % 2) * P
-            return planes[t // 2][:, first:first + P]
+            first = S + a * H + t * P
+            return planes[0][:, first:first + P]
 
         def w1_scale_of(a, t):
             return w1_scale[a][:, t * P:(t + 1) * P]
 
-        units = [(t + i, h) for t in range(0, PACK, 2) for h in range(HALVES) for i in range(2)]
+        units = [(t, h) for h in range(HALVES) for t in range(PACK)]
         size, damp = {}, {}
 
         def size_of_b(u):

@@ -45,11 +45,10 @@ def tile_list_rehab_embedding_refresh_kernel(
         picks = keep.tile([P, S // 16], U16, name="picks")
         places = keep.tile([P, S // 16], U16, name="places")
 
-        tab_rows = [held([P, T], U8, f"tab_rows{a}") for a in range(PASSES)]
+        tab_rows = held([P, PASSES, T], U8, "tab_rows")
         w2_rows = held([P, PASSES, H], U8, "w2_rows")
         nc.vector.memset(w2_rows[:].bitcast(I32), 0)
-        nc.vector.memset(tab_rows[0][:].bitcast(I32), 0)
-        nc.gpsimd.memset(tab_rows[1][:].bitcast(I32), 0)
+        nc.vector.memset(tab_rows[:].bitcast(I32), 0)
         planes = [held([P, S + PASSES * H], U8, "planes0"), held([P, S], U8, "planes1")]
         for h in range(HALVES):
             nc.vector.memset(planes[h][:].bitcast(I32), 0)
@@ -74,8 +73,9 @@ def tile_list_rehab_embedding_refresh_kernel(
         w2_raw = held([P, PASSES, 2 * H], U8, "w2_raw")
         nc.sync.dma_start(out=w2_raw[:].bitcast(I32), in_=w2_words.bitcast(I32).rearrange("a p c -> p a c"))
         nc.sync.dma_start(places[:], offs2)
-        for a in range(PASSES):
-            nc.sync.dma_start(out=tab_rows[a][32:96:4, :].bitcast(I32), in_=tab_scales[a].bitcast(I32))
+        nc.sync.dma_start(
+            out=tab_rows[32:96:4].bitcast(I32), in_=tab_scales.bitcast(I32).rearrange("a q c -> q a c")
+        )
 
         staged = held([P, S + PASSES * H], U8, "staged")
         nc.vector.tensor_copy(
@@ -91,7 +91,7 @@ def tile_list_rehab_embedding_refresh_kernel(
             for a in range(PASSES):
                 nc.vector.tensor_copy(
                     out=picked[h][:, a * BANK:(a + 1) * BANK],
-                    in_=tab_rows[a][:].indirect(picks[:, h * cols:(h + 1) * cols]),
+                    in_=tab_rows[:, a, :].indirect(picks[:, h * cols:(h + 1) * cols]),
                 )
             if h == 0:
                 nc.vector.tensor_copy(out=staged[:, :S].bitcast(I32), in_=picked[0][:].bitcast(I32))

@@ -49,6 +49,8 @@ def tile_list_rehab_embedding_refresh_kernel(
         w2_rows = held([P, PASSES, H], U8, "w2_rows")
         nc.vector.memset(w2_rows[:].bitcast(I32), 0)
         nc.vector.memset(tab_rows[:].bitcast(I32), 0)
+        identity = held([P, P], F32, "identity")
+        nc.vector.memset(identity[:], 0.0)
         planes = [held([P, S + PASSES * H], U8, "planes0"), held([P, S], U8, "planes1")]
         for h in range(HALVES):
             nc.vector.memset(planes[h][:].bitcast(I32), 0)
@@ -145,8 +147,7 @@ def tile_list_rehab_embedding_refresh_kernel(
             in_=w2_raw[:].bitcast(U16).rearrange("p a (m t) -> p a m t", t=PACK),
         )
 
-        identity = held([P, P], F32, "identity")
-        make_identity(nc, identity[:])
+        make_identity(nc, identity[:], nomemset=True)
         blocks = [slice(j0, j0 + P) for j0 in range(0, BANK, P)]
         flipped = psum.tile([P, BANK], F32, name="flipped", tag="bank7")
         for block in blocks:

@@ -62,9 +62,9 @@ def tile_list_rehab_embedding_refresh_kernel(
 
         tab = [held([P, T], U32, f"tab{a}") for a in range(PASSES)]
 
-        def load_table(a):
+        def load_table(a, part):
             words = tab_words[a].rearrange("p t i -> p (t i)").bitcast(I32)
-            nc.sync.dma_start(out=tab[a][:].bitcast(I32), in_=words)
+            nc.sync.dma_start(out=tab[a][:, part].bitcast(I32), in_=words[:, part])
 
         nc.sync.dma_start(picks[:], offs)
         gain_head = held([P, BANK], F32, "gain_head")
@@ -75,6 +75,7 @@ def tile_list_rehab_embedding_refresh_kernel(
         w2_raw = held([P, PASSES, 2 * H], U8, "w2_raw")
         nc.sync.dma_start(out=w2_raw[:].bitcast(I32), in_=w2_words.bitcast(I32).rearrange("a p c -> p a c"))
         nc.sync.dma_start(places[:], offs2)
+        load_table(0, slice(0, T // 16))
         nc.sync.dma_start(
             out=tab_rows[32:96:4].bitcast(I32), in_=tab_scales.bitcast(I32).rearrange("a q c -> q a c")
         )
@@ -104,8 +105,8 @@ def tile_list_rehab_embedding_refresh_kernel(
                     out=planes[h][r:P:32, :].bitcast(I32), in_=(staged, picked[1])[h][32 + 4 * r:96:16, :].bitcast(I32)
                 )
 
-        load_table(0)
-        load_table(1)
+        load_table(0, slice(T // 16, T))
+        load_table(1, slice(0, T))
         move_scale_rows(0)
 
         w1_raw = [held([P, PACK, H], F32, "w1_raw0"), reuse.tile([P, PACK, H], F32, name="w1_raw1", offset=0)]

from contextlib import ExitStack

import concourse.mybir as mybir
from concourse.masks import make_identity

K, T, S, T2, H, N = 1024, 4096, 1024, 2048, 512, 768
FLOPS = 2 * 2 * K * H * S + 2 * H * N * T2

F32 = mybir.dt.float32
BF16 = mybir.dt.bfloat16
I32 = mybir.dt.int32
U32 = mybir.dt.uint32
U16 = mybir.dt.uint16
U8 = mybir.dt.uint8
FP8X4 = mybir.dt.float8_e4m3fn_x4
FP4X4 = mybir.dt.float4_e2m1fn_x4
ACT = mybir.ActivationFunctionType
MULT = mybir.AluOpType.mult
ADD = mybir.AluOpType.add

P = 128
PACK = 4
PASSES = K // (P * PACK)
QUADS = 4
BANK = 512
HALVES = S // BANK
N_TILES = N // P


def tile_list_rehab_embedding_refresh_kernel(
    tc, tab_words, tab_scales, offs, offs2, w1, w2_words, w2_scales, wgs, page0,
    w3_words, w3_scales, b3, out_0, out_1, out_2, out_3,
):
    nc = tc.nc
    with ExitStack() as ctx:
        keep = ctx.enter_context(tc.tile_pool(name="keep", bufs=1))
        ring = ctx.enter_context(tc.tile_pool(name="ring", bufs=2))
        reuse = ctx.enter_context(tc.tile_pool(name="reuse", bufs=1))
        weaving = ctx.enter_context(tc.tile_pool(name="weaving", bufs=1))
        psum = ctx.enter_context(tc.psum_pool(name="psum", bufs=1))

        def held(shape, dtype, name):
            return keep.tile(shape, dtype, name=name, tag=name, align_bytes=64)

        picks = keep.tile([P, S // 16], U16, name="picks")
        places = keep.tile([P, S // 16], U16, name="places")

        tab_rows = held([P, PASSES, T], U8, "tab_rows")
        w2_rows = held([P, PASSES, H], U8, "w2_rows")
        nc.vector.memset(w2_rows[:].bitcast(I32), 0)
        nc.vector.memset(tab_rows[:].bitcast(I32), 0)
        identity = held([P, P], F32, "identity")
        nc.vector.memset(identity[:], 0.0)
        planes = [held([P, S + PASSES * H], U8, "planes0"), held([P, S], U8, "planes1")]
        for h in range(HALVES):
            nc.vector.memset(planes[h][:].bitcast(I32), 0)
        w3_scale = held([P, N], U8, "w3_scale")
        nc.vector.memset(w3_scale[:].bitcast(I32), 0)
        warm = held([P, 3], F32, "warm")
        nc.vector.memset(warm[:, 0:1], 1.0)
        nc.scalar.activation(out=warm[:, 1:2], in_=warm[:, 0:1], func=ACT.Abs_reciprocal_sqrt)

        tab = [held([P, T], U32, f"tab{a}") for a in range(PASSES)]

        def load_table(a, part):
            words = tab_words[a].rearrange("p t i -> p (t i)").bitcast(I32)
            nc.sync.dma_start(out=tab[a][:, part].bitcast(I32), in_=words[:, part])

        nc.sync.dma_start(picks[:], offs)
        gain_head = held([P, BANK], F32, "gain_head")
        nc.sync.dma_start(out=gain_head[:], in_=wgs[:, :BANK])
        nc.sync.dma_start(
            out=w2_rows[32:96:4].bitcast(I32), in_=w2_scales.bitcast(I32).rearrange("a q c -> q a c")
        )
        w2_raw = held([P, PASSES, 2 * H], U8, "w2_raw")
        nc.sync.dma_start(out=w2_raw[:].bitcast(I32), in_=w2_words.bitcast(I32).rearrange("a p c -> p a c"))
        nc.sync.dma_start(places[:], offs2)
        load_table(0, slice(0, T // 16))
        nc.sync.dma_start(
            out=tab_rows[32:96:4].bitcast(I32), in_=tab_scales.bitcast(I32).rearrange("a q c -> q a c")
        )

        staged = held([P, S + PASSES * H], U8, "staged")
        nc.vector.tensor_copy(
            out=staged[:, S:].rearrange("p (a t m) -> p a t m", a=PASSES, t=PACK),
            in_=w2_rows[:].rearrange("p a (m t) -> p a t m", t=PACK),
        )
        picked = [
            reuse.tile([P, S], U8, name="picked0", offset=9 * 1024 + BANK, align_bytes=64),
            held([P, S], U8, "picked1"),
        ]
        cols = BANK // 16
        for h in range(HALVES):
            for a in range(PASSES):
                nc.vector.tensor_copy(
                    out=picked[h][:, a * BANK:(a + 1) * BANK],
                    in_=tab_rows[:, a, :].indirect(picks[:, h * cols:(h + 1) * cols]),
                )
            if h == 0:
                nc.vector.tensor_copy(out=staged[:, :S].bitcast(I32), in_=picked[0][:].bitcast(I32))

        def move_scale_rows(h):
            for r in range(4):
                nc.sync.dma_start(
                    out=planes[h][r:P:32, :].bitcast(I32), in_=(staged, picked[1])[h][32 + 4 * r:96:16, :].bitcast(I32)
                )

        load_table(0, slice(T // 16, T))
        load_table(1, slice(0, T))
        move_scale_rows(0)

        w1_raw = [held([P, PACK, H], F32, "w1_raw0"), reuse.tile([P, PACK, H], F32, name="w1_raw1", offset=0)]
        w1_rows = w1.rearrange("(a p j) c -> a p j c", a=PASSES, j=PACK)
        gain = [held([P, PACK * BANK], F32, f"gain{h}") for h in range(HALVES)]
        gain_rows = wgs.rearrange("(q t) j -> q (t j)", t=PACK)

        def load_gain(t):
            for quad in (0, 2, 1, 3):
                nc.sync.dma_start(
                    out=gain[1][32 * quad:32 * quad + 32, t * BANK:(t + 1) * BANK],
                    in_=gain_rows[:, t * S + BANK:(t + 1) * S],
                )

        page = [held([P, T2], F32, f"page{t}") for t in range(PACK)]
        page_rows = page0.rearrange("(p t) c -> t p c", t=PACK)
        nc.sync.dma_start(out=w1_raw[0][:], in_=w1_rows[0])
        nc.sync.dma_start(out=w1_raw[1][:], in_=w1_rows[1])
        for t in range(PACK):
            nc.sync.dma_start(out=page[t][:], in_=page_rows[t])
            if t == 1:
                move_scale_rows(1)
        for t in range(PACK):
            load_gain(t)
        w3 = held([P, N], U32, "w3")
        nc.sync.dma_start(
            out=w3[:].bitcast(I32), in_=w3_words[0].rearrange("p c i -> p (c i)").bitcast(I32)
        )
        w3_scale_rows = w3_scales[0].bitcast(I32).rearrange("(Q r) c -> r Q c", r=4)
        for r in range(4):
            nc.sync.dma_start(out=w3_scale[r:P:32, :].bitcast(I32), in_=w3_scale_rows[r])
        bias = held([P, N_TILES], F32, "bias")
        with nc.allow_non_contiguous_dma(reason="one bias value to a partition"):
            nc.sync.dma_start(out=bias[:], in_=b3.rearrange("(i p) -> p i", p=P))

        w2 = held([P, PASSES, 2 * H], U8, "w2")
        nc.scalar.copy(
            out=w2[:].bitcast(U16).rearrange("p a (t m) -> p a m t", t=PACK),
            in_=w2_raw[:].bitcast(U16).rearrange("p a (m t) -> p a m t", t=PACK),
        )

        make_identity(nc, identity[:], nomemset=True)
        blocks = [slice(j0, j0 + P) for j0 in range(0, BANK, P)]
        flipped = psum.tile([P, BANK], F32, name="flipped", tag="bank7")
        for block in blocks:
            nc.tensor.transpose(flipped[:, block], gain_head[:, block], identity[:])
        dealt = held([P, len(blocks), PACK, P], F32, "dealt")
        for j, block in enumerate(blocks):
            rows = flipped[:, block].rearrange("p (q t) -> p t q", t=PACK)
            nc.scalar.copy(
                out=dealt[:, j].rearrange("p t (c q) -> p t c q", c=QUADS),
                in_=rows.unsqueeze(2).to_broadcast([P, PACK, QUADS, P // QUADS]),
            )
        for t in range(PACK):
            back = psum.tile([P, BANK], F32, name="back", tag=f"bank{5 + t % 2}")
            for j, block in enumerate(blocks):
                nc.tensor.transpose(back[:, block], dealt[:, j, t, :], identity[:])
            nc.scalar.copy(out=gain[0][:, t * BANK:(t + 1) * BANK], in_=back[:])

        v = [
            [reuse.tile([P, BANK], U32, name=f"v0_{h}", offset=(8 + 2 * h) * 1024, align_bytes=64) for h in range(HALVES)],
            [held([P, BANK], U32, f"v1_{h}") for h in range(HALVES)],
        ]
        for a in range(PASSES):
            for h in range(HALVES):
                nc.vector.tensor_copy(
                    out=v[a][h][:], in_=tab[a][:].indirect(picks[:, h * cols:(h + 1) * cols])
                )

        def product(words, scales, dtype, width, t, h, bank):
            acc = psum.tile([P, BANK], F32, name="acc", tag=f"bank{bank}")
            for a in range(PASSES):
                nc.tensor.matmul_mx(
                    out=acc[:],
                    lhsT=words[a][:, width * t * P:width * (t + 1) * P].bitcast(dtype),
                    lhsT_scale=scales(a, t),
                    rhs=v[a][h][:].bitcast(FP8X4),
                    rhs_scale=planes[h][:, a * BANK:(a + 1) * BANK],
                    start=(a == 0),
                    stop=(a == PASSES - 1),
                )
            return acc

        w2_passes = [w2[:, a, :] for a in range(PASSES)]

        def w2_scale_of(a, t):
            first = S + a * H + t * P
            return planes[0][:, first:first + P]

        def w1_scale_of(a, t):
            return w1_scale[a][:, t * P:(t + 1) * P]

        units = [(t, h) for h in range(HALVES) for t in range(PACK)]
        size, damp = {}, {}

        def size_of_b(u):
            acc_b = product(w2_passes, w2_scale_of, FP4X4, 2, *units[u], u % 5)
            size[u] = held([P, BANK], F32, "size")
            nc.scalar.activation(out=size[u][:], in_=acc_b[:], func=ACT.Abs)

        def inverse_root(u):
            if u == 1:
                damp[u] = reuse.tile([P, BANK], F32, name="second_damp", offset=0)
            else:
                damp[u] = ring.tile([P, BANK], F32, name="damp", bufs=2)
            nc.scalar.activation(out=damp[u][:], in_=size[u][:], func=ACT.Abs_reciprocal_sqrt, bias=1.0)

        def squared(u):
            nc.scalar.activation(out=damp[u][:], in_=damp[u][:], func=ACT.Square)

        size_of_b(0)
        inverse_root(0)
        size_of_b(1)
        squared(0)

        w1_codes = [held([P, H], U32, f"w1_codes{a}") for a in range(PASSES)]
        w1_scale = [held([P, H], U8, f"w1_scale{a}") for a in range(PASSES)]
        first_factor = reuse.tile([P, BANK], F32, name="first_factor", offset=4 * BANK)
        for a in range(PASSES):
            grouped = held([P, H * PACK], BF16, f"w1_grouped{a}")
            dst = grouped[:].rearrange("p (t m j) -> p m j t", t=PACK, j=PACK)
            src = w1_raw[a][:].rearrange("p j (m t) -> p m j t", t=PACK)
            if a == 0:
                nc.vector.tensor_copy(out=dst, in_=src)
            else:
                nc.vector.tensor_copy(out=dst[:, :, :, :2], in_=src[:, :, :, :2])
                nc.vector.tensor_copy(out=dst[:, :64, :, 2:], in_=src[:, :64, :, 2:])
                nc.scalar.copy(out=dst[:, 64:, :, 2:], in_=src[:, 64:, :, 2:])
                inverse_root(1)
            for c0, c1 in ((0, H),) if a == 0 else ((0, P), (P, 2 * P), (2 * P, H)):
                nc.vector.quantize_mx(
                    out=w1_codes[a][:, c0:c1].bitcast(FP8X4),
                    scales=w1_scale[a][:, c0:c1],
                    in_=grouped[:, PACK * c0:PACK * c1],
                )
                if a == 1 and c0 == P:
                    nc.vector.tensor_tensor(out=first_factor[:], in0=damp[0][:], in1=gain[0][:, :BANK], op=MULT)

        out_rows = out_1.rearrange("(p t) c -> t p c", t=PACK)
        for u, (t, h) in enumerate(units):
            fresh = held([P, BANK], F32, f"fresh{u}")[:]
            acc_a = product(w1_codes, w1_scale_of, FP8X4, 1, t, h, (u + 3) % 5)
            if u == 0:
                nc.vector.tensor_tensor(out=fresh, in0=acc_a[:], in1=first_factor[:], op=MULT)
            else:
                raw = ring.tile([P, BANK], F32, name="raw", bufs=4)
                if u == 1:
                    nc.scalar.copy(out=raw[:], in_=acc_a[:])
                    squared(u)
                    size_of_b(u + 1)
                    inverse_root(u + 1)
                else:
                    if u + 1 < len(units):
                        size_of_b(u + 1)
                    squared(u)
                    if u + 1 < len(units):
                        inverse_root(u + 1)
                    nc.scalar.copy(out=raw[:], in_=acc_a[:])
                partial = ring.tile([P, BANK], F32, name="partial", bufs=1)
                factors = (gain[h][:, t * BANK:(t + 1) * BANK], damp[u][:])
                nc.gpsimd.tensor_tensor(out=partial[:], in0=raw[:], in1=factors[u != 1], op=MULT)
                nc.gpsimd.tensor_tensor(out=fresh, in0=partial[:], in1=factors[u == 1], op=MULT)
            nc.vector.tensor_copy(out=page[t][:].indirect(places[:, h * cols:(h + 1) * cols]), in_=fresh)
            if h == HALVES - 1:
                nc.sync.dma_start(out=out_rows[t], in_=page[t][:])
        nc.scalar.activation(out=warm[:, 2:3], in_=damp[len(units) - 1][:, 0:1], func=ACT.Tanh)
        half = T2 // 2
        spans = ((0, BANK // 2), (BANK // 2, BANK), (BANK, half))
        pairs = keep.tile([P, 2 * half], F32, name="pairs", tag="size", align_bytes=64)
        rounded = ring.tile([P, PACK, half], BF16, name="rounded", tag="partial", bufs=1)

        def pair_words(c0, c1):
            return pairs[:, 2 * c0:2 * c1].rearrange("p (u c) -> p u c", u=2)

        def round_into_pairs(t, c0, c1):
            halves = pairs[:, 2 * c0:2 * c1].bitcast(BF16).rearrange("p (u c e) -> p u e c", u=2, e=2)
            nc.scalar.copy(out=halves[:, t // 2, t % 2, :], in_=page[t][:, c0:c1])

        for t in range(2):
            for c0, c1 in spans:
                round_into_pairs(t, c0, c1)
            nc.gpsimd.tensor_scalar(
                out=rounded[:, t, :], in0=page[t][:, half:], scalar1=1.0, scalar2=-0.0, op0=MULT, op1=ADD
            )
        for c0, c1 in spans:
            round_into_pairs(2, c0, c1)
        nc.scalar.copy(out=rounded[:, 2, :], in_=page[2][:, half:])
        for c0, c1 in spans:
            round_into_pairs(3, c0, c1)

        codes = held([P, T2], U32, "codes")
        scale = held([P, T2], U8, "scale")
        scale_rows = out_3[0].bitcast(I32)
        code_rows = out_2[0].rearrange("p c i -> p (c i)").bitcast(I32)

        def pack(woven, c0, c1):
            nc.vector.quantize_mx(out=codes[:, c0:c1].bitcast(FP8X4), scales=scale[:, c0:c1], in_=woven)

        for c0, c1 in spans:
            woven = weaving.tile([P, c1 - c0, 2], F32, name=f"woven{c0}", offset=8 * min(c0, BANK // 2), align_bytes=64)
            nc.vector.tensor_copy(out=woven[:], in_=pair_words(c0, c1).rearrange("p u c -> p c u"))
            pack(woven[:].rearrange("p c u -> p (c u)").bitcast(BF16), c0, c1)
        for c0 in range(0, half, BANK):
            woven = weaving.tile([P, BANK, PACK], BF16, name=f"late{c0}", offset=8 * c0, align_bytes=64)
            nc.vector.tensor_copy(out=rounded[:, 3, c0:c0 + BANK], in_=page[3][:, half + c0:half + c0 + BANK])
            nc.vector.tensor_copy(
                out=woven[:].rearrange("p (c i) t -> p c t i", i=4),
                in_=rounded[:, :, c0:c0 + BANK].rearrange("p t (c i) -> p c t i", i=4),
            )
            pack(woven[:].rearrange("p c t -> p (c t)"), half + c0, half + c0 + BANK)

        banks = list(range(8)) * 4
        out_tiles = out_0.rearrange("(i p) c -> p i c", p=P)

        def features(i, c0, c1, out):
            rows = slice(i * P, (i + 1) * P)
            acc_c = psum.tile([P, BANK], F32, name="acc_c", tag=f"bank{banks.pop()}")
            nc.tensor.matmul_mx(
                out=acc_c[:, :c1 - c0],
                lhsT=w3[:, rows].bitcast(FP8X4),
                lhsT_scale=w3_scale[:, rows],
                rhs=codes[:, c0:c1].bitcast(FP8X4),
                rhs_scale=scale[:, c0:c1],
                start=True,
                stop=True,
            )
            nc.scalar.activation(out=out, in_=acc_c[:, :c1 - c0], func=ACT.Tanh, bias=bias[:, i:i + 1])

        spaces = ("features", "tab1", "tab0")
        results = [keep.tile([P, 2 * T2], F32, name=f"features{i}", tag=spaces[i], align_bytes=64) for i in range(3)]

        def make(i, c0, c1):
            features(i, c0, c1, results[i // 2][:, i % 2 * T2 + c0:i % 2 * T2 + c1])

        def store(i, c0, c1):
            nc.sync.dma_start(out=out_tiles[:, i, c0:c1], in_=results[i // 2][:, i % 2 * T2 + c0:i % 2 * T2 + c1])

        def store_codes(c0, c1):
            nc.sync.dma_start(out=code_rows[:, c0:c1], in_=codes[:, c0:c1].bitcast(I32))

        for c0, c1 in spans[:2]:
            for i in range(2):
                make(i, c0, c1)
        store_codes(0, BANK)
        make(2, 0, BANK)
        for i in range(3):
            store(i, 0, BANK)
        store_codes(BANK, half)
        for i in range(3, N_TILES - 1):
            for c0 in range(0, half, BANK):
                make(i, c0, c0 + BANK)
            store(i, 0, half)
        store_codes(half, T2)
        for quad in range(QUADS):
            nc.gpsimd.dma_start(
                out=scale_rows[4 * quad:4 * quad + 4, :], in_=scale[32 * quad:32 * quad + 4, :].bitcast(I32)
            )
        for i, start in ((5, 0), (0, BANK), (1, BANK), (2, BANK), (3, half), (4, half)):
            for c0 in range(start, T2, BANK):
                make(i, c0, c0 + BANK)
            store(i, start, T2)
